import numpy as np
import ml_dtypes


def mxq(x, axis, fmt="e4m3"):
    dtype, down = {"e4m3": (ml_dtypes.float8_e4m3fn, 7), "e5m2": (ml_dtypes.float8_e5m2, 14)}[fmt]
    v = np.moveaxis(np.asarray(x, np.float32).astype(ml_dtypes.bfloat16).astype(np.float64), axis, -1)
    blocks = v.reshape(v.shape[:-1] + (-1, 32))
    amax = np.abs(blocks).max(-1, keepdims=True)
    byte = np.maximum(np.where(amax > 0, np.frexp(amax)[1] - 1 + 127, 0) - down, 1)
    scale = np.exp2(byte - 127.0)
    codes = (blocks / scale).astype(np.float32).astype(dtype).astype(np.float64)
    return np.moveaxis((codes * scale).reshape(v.shape), -1, axis)


WIDE = False


def mx_kscale(k):
    if not WIDE:
        return np.ones(k)
    levels = np.array([10, -10, 5, -5, 0])
    if k % 512:
        return np.exp2(np.random.permutation(np.resize(levels, k // 32))).repeat(32)
    a = np.empty((k // 512, 16))
    for p in range(k // 512):
        a[p, :8] = np.random.permutation(np.resize(levels, 8))
        for g in range(8):
            far = levels[np.abs(levels - a[p, g]) >= 10]
            a[p, g + 8] = far[np.random.randint(len(far))]
    return np.exp2(a.ravel()).repeat(32)


def f64(x):
    return np.asarray(x).astype(np.float64)


def striped(idx):
    return np.tile(idx.reshape(-1, 16).T, (8, 1)).astype(np.uint16)


def unstriped(offs):
    return offs[:16].T.reshape(-1).astype(np.int64)


def pack_weight(w):
    k, n = w.shape
    w = f64(np.asarray(w, np.float32).astype(ml_dtypes.bfloat16)).reshape(k // 32, 32, n)
    amax = np.abs(w).max(1)
    byte = np.clip(np.where(amax > 0, np.frexp(amax)[1] - 1 + 127 - 7, 1), 1, 254)
    scaled = (w * np.exp2(127.0 - byte)[:, None, :]).reshape(k, n).astype(np.float32)
    words = np.ascontiguousarray(scaled.reshape(k // 512, 128, 4, n).transpose(0, 1, 3, 2)).astype(ml_dtypes.float8_e4m3fn).view(np.uint8)
    return words, np.ascontiguousarray(byte.astype(np.uint8).reshape(k // 512, 16, n))


def unpack_weight(words, scales):
    g, p, n, _ = words.shape
    vals = np.ascontiguousarray(words).view(ml_dtypes.float8_e4m3fn).astype(np.float64) * np.repeat(np.exp2(scales.astype(np.float64) - 127.0), 8, axis=1)[..., None]
    return vals.transpose(0, 1, 3, 2).reshape(g * 512, n)

def planes(y):
    n, m = y.shape
    v = y.astype(np.float32).astype(ml_dtypes.bfloat16).astype(np.float64).reshape(n // 32, 32, m)
    top = np.abs(v).max(1)
    byte = np.clip(np.where(top > 0, np.frexp(top)[1] - 1 + 127 - 7, 1), 1, 254)
    codes = (v * np.exp2(127.0 - byte)[:, None, :]).reshape(n, m).astype(np.float32).astype(ml_dtypes.float8_e4m3fn).view(np.uint8)
    words = codes.reshape(n // 512, 128, 4, m).transpose(0, 1, 3, 2)
    return np.ascontiguousarray(words), np.ascontiguousarray(byte.astype(np.uint8).reshape(n // 512, 16, m))


K, T, S, V, H = 512, 1024, 512, 128, 512


def setup_inputs():
    n = np.random.standard_normal
    s = mx_kscale(K)[:, None]
    u = mx_kscale(H)
    packed_xT = pack_weight(n((K, T)) * s)
    packed_w2 = pack_weight(n((H, H)) / np.sqrt(2 * H) / u[:, None])
    packed_w3 = pack_weight(n((H, H)) / np.sqrt(2 * H) / u[:, None])
    return {
        "x_words": packed_xT[0],
        "x_scales": packed_xT[1],
        "w1": (n((K, H)) / np.sqrt(K) / s * u).astype(np.float32),
        "w2_words": packed_w2[0],
        "w2_scales": packed_w2[1],
        "w3_words": packed_w3[0],
        "w3_scales": packed_w3[1],
        "offs": striped(np.random.permutation(T)[:S]),
    }


def reference(x_words, x_scales, w1, w2_words, w2_scales, w3_words, w3_scales, offs):
    xq = unpack_weight(x_words, x_scales)[:, unstriped(offs)]
    h = mxq(f64(w1), 0, "e4m3").T @ xq
    mean = (h[:, :V] + h[:, V:2 * V] + h[:, 2 * V:3 * V] + h[:, 3 * V:4 * V]) / 4
    dev = np.sqrt(((h[:, :V] - mean) ** 2 + (h[:, V:2 * V] - mean) ** 2 + (h[:, 2 * V:3 * V] - mean) ** 2 + (h[:, 3 * V:4 * V] - mean) ** 2) / 4)
    out_0 = unpack_weight(w2_words, w2_scales).T @ mxq(mean, 0, "e4m3") + unpack_weight(w3_words, w3_scales).T @ mxq(dev, 0, "e4m3")
    return (out_0,) + planes(out_0)

@@ -1,0 +1,187 @@
+from contextlib import ExitStack
+
+import concourse.mybir as mybir
+
+K, T, S, V, H = 512, 1024, 512, 128, 512
+FLOPS = 2 * K * H * S + 2 * 2 * H * H * V
+
+F32 = mybir.dt.float32
+BF16 = mybir.dt.bfloat16
+I32 = mybir.dt.int32
+U32 = mybir.dt.uint32
+U16 = mybir.dt.uint16
+U8 = mybir.dt.uint8
+FP8X4 = mybir.dt.float8_e4m3fn_x4
+ACT = mybir.ActivationFunctionType
+MULT = mybir.AluOpType.mult
+ADD = mybir.AluOpType.add
+
+P = 128
+PACK = 4
+PIECES = 4
+QUADS = 4
+
+
+def words_of(dram):
+    return dram[0].rearrange("p n r -> p (n r)").bitcast(I32)
+
+
+def tile_picked_statpool_none_po_kernel(
+    tc, x_words, x_scales, w1, w2_words, w2_scales, w3_words, w3_scales, offs, out_0, out_1, out_2
+):
+    nc = tc.nc
+    with ExitStack() as ctx:
+        sb = ctx.enter_context(tc.tile_pool(name="sb", bufs=1))
+        ps = ctx.enter_context(tc.psum_pool(name="ps", bufs=1))
+
+        def tile(shape, dtype, name):
+            return sb.tile(shape, dtype, name=name, align_bytes=64)
+
+        offsets = sb.tile([P, S // 16], U16, name="offsets")
+        x_scale_tab = tile([P, T], U8, "x_scale_tab")
+        w_scale_raw = tile([P, H], U8, "w_scale_raw")
+        one = tile([P, 1], F32, "one")
+        root = sb.tile([P, 1], F32, name="root", tag="late", align_bytes=64)
+        nc.vector.memset(x_scale_tab[:].bitcast(I32), 0)
+        nc.vector.memset(one[:], 1.0)
+        nc.vector.memset(w_scale_raw[:].bitcast(I32), 0)
+
+        nc.sync.dma_start(offsets[:], offs)
+        for q in range(QUADS):
+            nc.scalar.dma_start(
+                x_scale_tab[32 * q : 32 * q + 4, :].bitcast(I32), x_scales[0, 4 * q : 4 * q + 4, :].bitcast(I32)
+            )
+        nc.scalar.activation(root[:], one[:], ACT.Sqrt)
+        HALF = H // 2
+        w1_rows = w1.rearrange("(p j) c -> p j c", j=PACK)
+        w1_raw = [tile([P, PACK, HALF], F32, f"w1_raw{h}") for h in range(2)]
+        for h in range(2):
+            nc.sync.dma_start(w1_raw[h][:], w1_rows[:, :, h * HALF : (h + 1) * HALF])
+        x_word_tab = tile([P, T], I32, "x_word_tab")
+        nc.sync.dma_start(x_word_tab[:], words_of(x_words))
+        w_words = sb.tile([P, 2 * H], I32, name="w_words", tag="late", align_bytes=64)
+        w_word_raw = [w_words[:, u * H : (u + 1) * H] for u in range(2)]
+        for u, (words, scales) in enumerate(((w2_words, w2_scales), (w3_words, w3_scales))):
+            nc.sync.dma_start(w_word_raw[u], words_of(words))
+        for u, (words, scales) in enumerate(((w2_words, w2_scales), (w3_words, w3_scales))):
+            for q in range(QUADS):
+                r = 32 * q + 4 * u
+                nc.sync.dma_start(
+                    w_scale_raw[r : r + 4, :].bitcast(I32), scales[0, 4 * q : 4 * q + 4, :].bitcast(I32)
+                )
+
+        x_scale = tile([P, S], U8, "x_scale")
+        nc.vector.tensor_copy(x_scale[:], x_scale_tab[:].indirect(offsets[:]))
+
+        w1_bf = tile([P, PACK * H], BF16, "w1_bf")
+        dealt = w1_bf[:].rearrange("p (t m j) -> p m j t", t=4, j=PACK)
+        SPLIT = 44
+        src0 = w1_raw[0][:].rearrange("p j (m t) -> p m j t", t=4)
+        src1 = w1_raw[1][:].rearrange("p j (m t) -> p m j t", t=4)
+        nc.scalar.copy(dealt[:, 0:64], src0)
+        nc.vector.tensor_copy(dealt[:, 64 : 64 + SPLIT], src1[:, 0:SPLIT])
+        nc.scalar.copy(dealt[:, 64 + SPLIT : 128], src1[:, SPLIT:64])
+        w1_code = [tile([P, P], U32, f"w1_code{t}") for t in range(4)]
+        w1_scale = [tile([P, P], U8, f"w1_scale{t}") for t in range(4)]
+        for t in range(4):
+            nc.vector.quantize_mx(w1_code[t][:].bitcast(FP8X4), w1_scale[t][:], w1_bf[:, t * H : (t + 1) * H])
+
+        h_bank = []
+        for d in range(PIECES):
+            x_code = tile([P, V], U32, f"x_code{d}")
+            nc.vector.tensor_copy(x_code[:], x_word_tab[:].bitcast(U32).indirect(offsets[:, 8 * d : 8 * d + 8]))
+            bank = ps.tile([P, 4 * V], F32, name=f"h{d}")
+            for t in range(4):
+                nc.tensor.matmul_mx(
+                    bank[:, t * V : (t + 1) * V],
+                    lhsT=w1_code[t][:].bitcast(FP8X4),
+                    lhsT_scale=w1_scale[t][:],
+                    rhs=x_code[:].bitcast(FP8X4),
+                    rhs_scale=x_scale[:, d * V : (d + 1) * V],
+                    start=True,
+                    stop=True,
+                )
+            h_bank.append(bank[:].rearrange("p (t v) -> p v t", t=4))
+
+        w_code = [tile([P, H], I32, f"w_code{u}") for u in range(2)]
+        w_scale = tile([P, H], U8, "w_scale")
+
+        def deal(dst, src):
+            nc.vector.tensor_copy(dst.rearrange("p (t m) -> p m t", t=4), src.rearrange("p (m t) -> p m t", t=4))
+
+        deal(w_code[0][:], w_word_raw[0])
+
+        def woven(name, dtype=F32):
+            return tile([P, 4 * V], dtype, name)
+
+        def vt(x):
+            return x[:].rearrange("p (v t) -> p v t", t=4)
+
+        def step(out, d, c, prev, vs=slice(0, V)):
+            nc.vector.scalar_tensor_tensor(vt(out)[:, vs], h_bank[d][:, vs], c, vt(prev)[:, vs], MULT, ADD)
+
+        halves = (slice(0, V // 2), slice(V // 2, V))
+        s1, s2, s3 = woven("s1"), woven("s2"), woven("s3")
+        c1, c2, c3 = woven("c1"), woven("c2"), woven("c3")
+        q1, q2, q3, q12, var = woven("q1"), woven("q2"), woven("q3"), woven("q12"), woven("var")
+        mean_bf, dev_bf = woven("mean_bf", BF16), woven("dev_bf", BF16)
+        nc.scalar.activation(vt(s1), h_bank[0], ACT.Copy, scale=0.25)
+        step(s2, 1, 0.25, s1)
+        step(c1, 1, -0.25, s1)
+        nc.scalar.activation(q1[:], c1[:], ACT.Square, scale=2.0**0.5)
+        for vs in halves:
+            step(c2, 2, -0.5, s2, vs)
+            nc.scalar.activation(vt(q2)[:, vs], vt(c2)[:, vs], ACT.Square, scale=(2.0 / 3.0) ** 0.5)
+            nc.gpsimd.tensor_tensor(vt(q12)[:, vs], vt(q1)[:, vs], vt(q2)[:, vs], ADD)
+        for vs in halves:
+            step(s3, 2, 0.25, s2, vs)
+        for vs in halves:
+            step(c3, 3, -0.75, s3, vs)
+            nc.scalar.activation(vt(q3)[:, vs], vt(c3)[:, vs], ACT.Square, scale=(1.0 / 3.0) ** 0.5)
+        step(mean_bf, 3, 0.25, s3)
+        deal(w_scale[:], w_scale_raw[:])
+        for vs in halves:
+            nc.vector.tensor_tensor(vt(var)[:, vs], vt(q12)[:, vs], vt(q3)[:, vs], ADD)
+            nc.scalar.activation(vt(dev_bf)[:, vs], vt(var)[:, vs], ACT.Sqrt)
+        stat_code = [tile([P, V], U32, f"stat_code{u}") for u in range(2)]
+        stat_scale = [tile([P, V], U8, f"stat_scale{u}") for u in range(2)]
+        nc.vector.quantize_mx(stat_code[0][:].bitcast(FP8X4), stat_scale[0][:], mean_bf[:])
+        deal(w_code[1][:], w_word_raw[1])
+        for vs in halves:
+            nc.vector.quantize_mx(
+                stat_code[1][:, vs].bitcast(FP8X4), stat_scale[1][:, vs], dev_bf[:, 4 * vs.start : 4 * vs.stop]
+            )
+
+        y_bank = [ps.tile([P, V], F32, name=f"y{t}") for t in range(4)]
+        y = tile([P, 4, V], F32, "y")
+        for u in range(2):
+            for t in range(4):
+                nc.tensor.matmul_mx(
+                    y_bank[t][:],
+                    lhsT=w_code[u][:, t * P : (t + 1) * P].bitcast(FP8X4),
+                    lhsT_scale=w_scale[4 * u : P, t * P : (t + 1) * P],
+                    rhs=stat_code[u][:].bitcast(FP8X4),
+                    rhs_scale=stat_scale[u][:],
+                    start=(u == 0),
+                    stop=(u == 1),
+                )
+        for t in range(4):
+            nc.scalar.copy(y[:, t, :], y_bank[t][:])
+        nc.scalar.dma_start(out_0.rearrange("(p t) v -> p t v", t=4), y[:])
+
+        y_bf = woven("y_bf", BF16)
+        for vs in halves:
+            nc.vector.tensor_copy(
+                y_bf[:, 4 * vs.start : 4 * vs.stop].rearrange("p (c i t) -> p c t i", i=4, t=4),
+                y[:, :, vs].rearrange("p t (c i) -> p c t i", i=4),
+            )
+        y_code = tile([P, V], I32, "y_code")
+        y_scale = tile([P, V], U8, "y_scale")
+        for vs in halves:
+            nc.vector.quantize_mx(
+                y_code[:, vs].bitcast(FP8X4), y_scale[:, vs], y_bf[:, 4 * vs.start : 4 * vs.stop]
+            )
+        nc.sync.dma_start(words_of(out_1), y_code[:])
+        for q in range(QUADS):
+            eng = nc.sync if q < 2 else nc.scalar
+            eng.dma_start(out_2[0, 4 * q : 4 * q + 4, :].bitcast(I32), y_scale[32 * q : 32 * q + 4, :].bitcast(I32))

@@ -47,6 +47,8 @@ def tile_picked_statpool_none_po_kernel(
         nc.vector.memset(w_scale_raw[:].bitcast(I32), 0)
 
         nc.sync.dma_start(offsets[:], offs)
+        x_word_tab = tile([P, T], I32, "x_word_tab")
+        nc.sync.dma_start(x_word_tab[:], words_of(x_words))
         for q in range(QUADS):
             nc.scalar.dma_start(
                 x_scale_tab[32 * q : 32 * q + 4, :].bitcast(I32), x_scales[0, 4 * q : 4 * q + 4, :].bitcast(I32)
@@ -57,8 +59,6 @@ def tile_picked_statpool_none_po_kernel(
         w1_raw = [tile([P, PACK, HALF], F32, f"w1_raw{h}") for h in range(2)]
         for h in range(2):
             nc.sync.dma_start(w1_raw[h][:], w1_rows[:, :, h * HALF : (h + 1) * HALF])
-        x_word_tab = tile([P, T], I32, "x_word_tab")
-        nc.sync.dma_start(x_word_tab[:], words_of(x_words))
         w_words = sb.tile([P, 2 * H], I32, name="w_words", tag="late", align_bytes=64)
         w_word_raw = [w_words[:, u * H : (u + 1) * H] for u in range(2)]
         for u, (words, scales) in enumerate(((w2_words, w2_scales), (w3_words, w3_scales))):
@@ -70,14 +70,16 @@ def tile_picked_statpool_none_po_kernel(
                     w_scale_raw[r : r + 4, :].bitcast(I32), scales[0, 4 * q : 4 * q + 4, :].bitcast(I32)
                 )
 
+        x_code = tile([P, S], U32, "x_code")
+        nc.vector.tensor_copy(x_code[:], x_word_tab[:].bitcast(U32).indirect(offsets[:]))
         x_scale = tile([P, S], U8, "x_scale")
         nc.vector.tensor_copy(x_scale[:], x_scale_tab[:].indirect(offsets[:]))
 
         w1_bf = tile([P, PACK * H], BF16, "w1_bf")
-        dealt = w1_bf[:].rearrange("p (t m j) -> p m j t", t=4, j=PACK)
+        dealt = w1_bf[:].rearrange("p (t m j) -> p m t j", t=4, j=PACK)
         SPLIT = 44
-        src0 = w1_raw[0][:].rearrange("p j (m t) -> p m j t", t=4)
-        src1 = w1_raw[1][:].rearrange("p j (m t) -> p m j t", t=4)
+        src0 = w1_raw[0][:].rearrange("p j (m t) -> p m t j", t=4)
+        src1 = w1_raw[1][:].rearrange("p j (m t) -> p m t j", t=4)
         nc.scalar.copy(dealt[:, 0:64], src0)
         nc.vector.tensor_copy(dealt[:, 64 : 64 + SPLIT], src1[:, 0:SPLIT])
         nc.scalar.copy(dealt[:, 64 + SPLIT : 128], src1[:, SPLIT:64])
@@ -88,15 +90,13 @@ def tile_picked_statpool_none_po_kernel(
 
         h_bank = []
         for d in range(PIECES):
-            x_code = tile([P, V], U32, f"x_code{d}")
-            nc.vector.tensor_copy(x_code[:], x_word_tab[:].bitcast(U32).indirect(offsets[:, 8 * d : 8 * d + 8]))
             bank = ps.tile([P, 4 * V], F32, name=f"h{d}")
             for t in range(4):
                 nc.tensor.matmul_mx(
                     bank[:, t * V : (t + 1) * V],
                     lhsT=w1_code[t][:].bitcast(FP8X4),
                     lhsT_scale=w1_scale[t][:],
-                    rhs=x_code[:].bitcast(FP8X4),
+                    rhs=x_code[:, d * V : (d + 1) * V].bitcast(FP8X4),
                     rhs_scale=x_scale[:, d * V : (d + 1) * V],
                     start=True,
                     stop=True,
@@ -107,9 +107,12 @@ def tile_picked_statpool_none_po_kernel(
         w_scale = tile([P, H], U8, "w_scale")
 
         def deal(dst, src):
-            nc.vector.tensor_copy(dst.rearrange("p (t m) -> p m t", t=4), src.rearrange("p (m t) -> p m t", t=4))
+            nc.vector.tensor_copy(
+                dst.rearrange("p (t b i) -> p b t i", t=4, i=4), src.rearrange("p (b i t) -> p b t i", t=4, i=4)
+            )
 
         deal(w_code[0][:], w_word_raw[0])
+        deal(w_code[1][:], w_word_raw[1])
 
         def woven(name, dtype=F32):
             return tile([P, 4 * V], dtype, name)
@@ -132,21 +135,25 @@ def tile_picked_statpool_none_po_kernel(
         for vs in halves:
             step(c2, 2, -0.5, s2, vs)
             nc.scalar.activation(vt(q2)[:, vs], vt(c2)[:, vs], ACT.Square, scale=(2.0 / 3.0) ** 0.5)
-            nc.gpsimd.tensor_tensor(vt(q12)[:, vs], vt(q1)[:, vs], vt(q2)[:, vs], ADD)
+        late = halves[1]
+        nc.gpsimd.tensor_tensor(vt(q12)[:, late], vt(q1)[:, late], vt(q2)[:, late], ADD)
         for vs in halves:
             step(s3, 2, 0.25, s2, vs)
         for vs in halves:
             step(c3, 3, -0.75, s3, vs)
             nc.scalar.activation(vt(q3)[:, vs], vt(c3)[:, vs], ACT.Square, scale=(1.0 / 3.0) ** 0.5)
         step(mean_bf, 3, 0.25, s3)
-        deal(w_scale[:], w_scale_raw[:])
-        for vs in halves:
-            nc.vector.tensor_tensor(vt(var)[:, vs], vt(q12)[:, vs], vt(q3)[:, vs], ADD)
-            nc.scalar.activation(vt(dev_bf)[:, vs], vt(var)[:, vs], ACT.Sqrt)
+        nc.vector.tensor_copy(
+            w_scale[:].rearrange("p (t m) -> p t m", t=4), w_scale_raw[:].rearrange("p (m t) -> p t m", t=4)
+        )
+        early = halves[0]
+        nc.vector.tensor_tensor(vt(q12)[:, early], vt(q1)[:, early], vt(q2)[:, early], ADD)
         stat_code = [tile([P, V], U32, f"stat_code{u}") for u in range(2)]
         stat_scale = [tile([P, V], U8, f"stat_scale{u}") for u in range(2)]
         nc.vector.quantize_mx(stat_code[0][:].bitcast(FP8X4), stat_scale[0][:], mean_bf[:])
-        deal(w_code[1][:], w_word_raw[1])
+        for vs in halves:
+            nc.vector.tensor_tensor(vt(var)[:, vs], vt(q12)[:, vs], vt(q3)[:, vs], ADD)
+            nc.scalar.activation(vt(dev_bf)[:, vs], vt(var)[:, vs], ACT.Sqrt)
         for vs in halves:
             nc.vector.quantize_mx(
                 stat_code[1][:, vs].bitcast(FP8X4), stat_scale[1][:, vs], dev_bf[:, 4 * vs.start : 4 * vs.stop]

@@ -39,27 +39,27 @@ def tile_picked_statpool_none_po_kernel(
 
         offsets = sb.tile([P, S // 16], U16, name="offsets")
         x_scale_tab = tile([P, T], U8, "x_scale_tab")
-        w_scale_raw = tile([P, H], U8, "w_scale_raw")
-        one = tile([P, 1], F32, "one")
-        root = sb.tile([P, 1], F32, name="root", tag="late", align_bytes=64)
+        w_scale_raw = sb.tile([P, H], U8, name="w_scale_raw", tag="scale_then_sum", align_bytes=64)
+        two = tile([P, 1], F32, "two")
+        root_two = tile([P, 1], F32, "root_two")
         nc.vector.memset(x_scale_tab[:].bitcast(I32), 0)
-        nc.vector.memset(one[:], 1.0)
+        nc.vector.memset(two[:], 2.0)
         nc.vector.memset(w_scale_raw[:].bitcast(I32), 0)
 
         nc.sync.dma_start(offsets[:], offs)
         x_word_tab = tile([P, T], I32, "x_word_tab")
         nc.sync.dma_start(x_word_tab[:], words_of(x_words))
         for q in range(QUADS):
-            nc.scalar.dma_start(
+            nc.sync.dma_start(
                 x_scale_tab[32 * q : 32 * q + 4, :].bitcast(I32), x_scales[0, 4 * q : 4 * q + 4, :].bitcast(I32)
             )
-        nc.scalar.activation(root[:], one[:], ACT.Sqrt)
+        nc.scalar.activation(root_two[:], two[:], ACT.Sqrt)
         HALF = H // 2
         w1_rows = w1.rearrange("(p j) c -> p j c", j=PACK)
         w1_raw = [tile([P, PACK, HALF], F32, f"w1_raw{h}") for h in range(2)]
         for h in range(2):
             nc.sync.dma_start(w1_raw[h][:], w1_rows[:, :, h * HALF : (h + 1) * HALF])
-        w_words = sb.tile([P, 2 * H], I32, name="w_words", tag="late", align_bytes=64)
+        w_words = sb.tile([P, 2 * H], I32, name="w_words", tag="words_then_pair", align_bytes=64)
         w_word_raw = [w_words[:, u * H : (u + 1) * H] for u in range(2)]
         for u, (words, scales) in enumerate(((w2_words, w2_scales), (w3_words, w3_scales))):
             nc.sync.dma_start(w_word_raw[u], words_of(words))
@@ -75,18 +75,22 @@ def tile_picked_statpool_none_po_kernel(
         x_scale = tile([P, S], U8, "x_scale")
         nc.vector.tensor_copy(x_scale[:], x_scale_tab[:].indirect(offsets[:]))
 
-        w1_bf = tile([P, PACK * H], BF16, "w1_bf")
-        dealt = w1_bf[:].rearrange("p (t m j) -> p m t j", t=4, j=PACK)
-        SPLIT = 44
+        w1_bf = [tile([P, PACK * HALF], BF16, f"w1_bf{h}") for h in range(2)]
+        dealt = [x[:].rearrange("p (t m j) -> p m t j", t=4, j=PACK) for x in w1_bf]
+        SPLIT = 48
         src0 = w1_raw[0][:].rearrange("p j (m t) -> p m t j", t=4)
         src1 = w1_raw[1][:].rearrange("p j (m t) -> p m t j", t=4)
-        nc.scalar.copy(dealt[:, 0:64], src0)
-        nc.vector.tensor_copy(dealt[:, 64 : 64 + SPLIT], src1[:, 0:SPLIT])
-        nc.scalar.copy(dealt[:, 64 + SPLIT : 128], src1[:, SPLIT:64])
+        nc.scalar.copy(dealt[0], src0)
+        nc.vector.tensor_copy(dealt[1][:, 0:SPLIT], src1[:, 0:SPLIT])
+        nc.scalar.copy(dealt[1][:, SPLIT:64], src1[:, SPLIT:64])
         w1_code = [tile([P, P], U32, f"w1_code{t}") for t in range(4)]
         w1_scale = [tile([P, P], U8, f"w1_scale{t}") for t in range(4)]
-        for t in range(4):
-            nc.vector.quantize_mx(w1_code[t][:].bitcast(FP8X4), w1_scale[t][:], w1_bf[:, t * H : (t + 1) * H])
+        for h in range(2):
+            ms = slice(64 * h, 64 * h + 64)
+            for t in range(4):
+                nc.vector.quantize_mx(
+                    w1_code[t][:, ms].bitcast(FP8X4), w1_scale[t][:, ms], w1_bf[h][:, t * HALF : (t + 1) * HALF]
+                )
 
         h_bank = []
         for d in range(PIECES):
@@ -113,47 +117,53 @@ def tile_picked_statpool_none_po_kernel(
 
         deal(w_code[0][:], w_word_raw[0])
         deal(w_code[1][:], w_word_raw[1])
+        nc.gpsimd.tensor_copy(
+            w_scale[:].rearrange("p (t m) -> p t m", t=4), w_scale_raw[:].rearrange("p (m t) -> p t m", t=4)
+        )
 
         def woven(name, dtype=F32):
             return tile([P, 4 * V], dtype, name)
 
         def vt(x):
-            return x[:].rearrange("p (v t) -> p v t", t=4)
+            return x[:, :].rearrange("p (v t) -> p v t", t=4)
 
         def step(out, d, c, prev, vs=slice(0, V)):
             nc.vector.scalar_tensor_tensor(vt(out)[:, vs], h_bank[d][:, vs], c, vt(prev)[:, vs], MULT, ADD)
 
         halves = (slice(0, V // 2), slice(V // 2, V))
-        s1, s2, s3 = woven("s1"), woven("s2"), woven("s3")
-        c1, c2, c3 = woven("c1"), woven("c2"), woven("c3")
-        q1, q2, q3, q12, var = woven("q1"), woven("q2"), woven("q3"), woven("q12"), woven("var")
+        s1, s3 = woven("s1"), woven("s3")
+        pair = sb.tile([P, 8 * V], F32, name="pair", tag="words_then_pair", align_bytes=64)
+        s2, c1 = pair[:, 0 : 4 * V], pair[:, 4 * V : 8 * V]
+        c2, c3 = woven("c2"), woven("c3")
+        q1, q2, q3, var = woven("q1"), woven("q2"), woven("q3"), woven("var")
+        q12 = sb.tile([P, 4 * V], F32, name="q12", tag="scale_then_sum", align_bytes=64)
         mean_bf, dev_bf = woven("mean_bf", BF16), woven("dev_bf", BF16)
-        nc.scalar.activation(vt(s1), h_bank[0], ACT.Copy, scale=0.25)
-        step(s2, 1, 0.25, s1)
-        step(c1, 1, -0.25, s1)
-        nc.scalar.activation(q1[:], c1[:], ACT.Square, scale=2.0**0.5)
+        for vs in halves:
+            nc.scalar.activation(vt(s1)[:, vs], h_bank[0][:, vs], ACT.Copy, scale=0.25)
+            step(s2, 1, 0.25, s1, vs)
+        for vs in halves:
+            step(c1, 1, -0.25, s1, vs)
+            nc.scalar.activation(vt(q1)[:, vs], vt(c1)[:, vs], ACT.Square, scale=root_two[:])
         for vs in halves:
             step(c2, 2, -0.5, s2, vs)
             nc.scalar.activation(vt(q2)[:, vs], vt(c2)[:, vs], ACT.Square, scale=(2.0 / 3.0) ** 0.5)
-        late = halves[1]
-        nc.gpsimd.tensor_tensor(vt(q12)[:, late], vt(q1)[:, late], vt(q2)[:, late], ADD)
+        for vs in halves:
+            nc.gpsimd.tensor_tensor(vt(q12)[:, vs], vt(q1)[:, vs], vt(q2)[:, vs], ADD)
         for vs in halves:
             step(s3, 2, 0.25, s2, vs)
         for vs in halves:
             step(c3, 3, -0.75, s3, vs)
             nc.scalar.activation(vt(q3)[:, vs], vt(c3)[:, vs], ACT.Square, scale=(1.0 / 3.0) ** 0.5)
         step(mean_bf, 3, 0.25, s3)
-        nc.vector.tensor_copy(
-            w_scale[:].rearrange("p (t m) -> p t m", t=4), w_scale_raw[:].rearrange("p (m t) -> p t m", t=4)
-        )
-        early = halves[0]
-        nc.vector.tensor_tensor(vt(q12)[:, early], vt(q1)[:, early], vt(q2)[:, early], ADD)
-        stat_code = [tile([P, V], U32, f"stat_code{u}") for u in range(2)]
-        stat_scale = [tile([P, V], U8, f"stat_scale{u}") for u in range(2)]
-        nc.vector.quantize_mx(stat_code[0][:].bitcast(FP8X4), stat_scale[0][:], mean_bf[:])
         for vs in halves:
             nc.vector.tensor_tensor(vt(var)[:, vs], vt(q12)[:, vs], vt(q3)[:, vs], ADD)
             nc.scalar.activation(vt(dev_bf)[:, vs], vt(var)[:, vs], ACT.Sqrt)
+        stat_code = [
+            sb.tile([P, V], U32, name="mean_code", tag="scale_then_sum", align_bytes=64),
+            tile([P, V], U32, "dev_code"),
+        ]
+        stat_scale = [tile([P, V], U8, f"stat_scale{u}") for u in range(2)]
+        nc.vector.quantize_mx(stat_code[0][:].bitcast(FP8X4), stat_scale[0][:], mean_bf[:])
         for vs in halves:
             nc.vector.quantize_mx(
                 stat_code[1][:, vs].bitcast(FP8X4), stat_scale[1][:, vs], dev_bf[:, 4 * vs.start : 4 * vs.stop]

@@ -46,21 +46,20 @@ def tile_picked_statpool_none_po_kernel(
         nc.vector.memset(two[:], 2.0)
         nc.vector.memset(w_scale_raw[:].bitcast(I32), 0)
 
+        HALF = H // 2
+        w1_rows = w1.rearrange("(p j) c -> p j c", j=PACK)
+        w1_raw = [tile([P, PACK, HALF], F32, f"w1_raw{h}") for h in range(2)]
+        nc.sync.dma_start(w1_raw[0][:], w1_rows[:, :, 0:HALF])
         nc.sync.dma_start(offsets[:], offs)
-        x_word_tab = tile([P, T], I32, "x_word_tab")
-        nc.sync.dma_start(x_word_tab[:], words_of(x_words))
         for q in range(QUADS):
             nc.sync.dma_start(
                 x_scale_tab[32 * q : 32 * q + 4, :].bitcast(I32), x_scales[0, 4 * q : 4 * q + 4, :].bitcast(I32)
             )
         nc.scalar.activation(root_two[:], two[:], ACT.Sqrt)
-        HALF = H // 2
-        w1_rows = w1.rearrange("(p j) c -> p j c", j=PACK)
-        w1_raw = [tile([P, PACK, HALF], F32, f"w1_raw{h}") for h in range(2)]
-        for h in range(2):
-            nc.sync.dma_start(w1_raw[h][:], w1_rows[:, :, h * HALF : (h + 1) * HALF])
-        w_words = sb.tile([P, 2 * H], I32, name="w_words", tag="words_then_pair", align_bytes=64)
-        w_word_raw = [w_words[:, u * H : (u + 1) * H] for u in range(2)]
+        nc.sync.dma_start(w1_raw[1][:], w1_rows[:, :, HALF:H])
+        x_word_tab = sb.tile([P, T], I32, name="x_word_tab", tag="table_then_codes", align_bytes=64)
+        nc.sync.dma_start(x_word_tab[:], words_of(x_words))
+        w_word_raw = [tile([P, H], I32, f"w_word_raw{u}")[:] for u in range(2)]
         for u, (words, scales) in enumerate(((w2_words, w2_scales), (w3_words, w3_scales))):
             nc.sync.dma_start(w_word_raw[u], words_of(words))
         for u, (words, scales) in enumerate(((w2_words, w2_scales), (w3_words, w3_scales))):
@@ -70,28 +69,28 @@ def tile_picked_statpool_none_po_kernel(
                     w_scale_raw[r : r + 4, :].bitcast(I32), scales[0, 4 * q : 4 * q + 4, :].bitcast(I32)
                 )
 
-        x_code = tile([P, S], U32, "x_code")
-        nc.vector.tensor_copy(x_code[:], x_word_tab[:].bitcast(U32).indirect(offsets[:]))
         x_scale = tile([P, S], U8, "x_scale")
         nc.vector.tensor_copy(x_scale[:], x_scale_tab[:].indirect(offsets[:]))
 
-        w1_bf = [tile([P, PACK * HALF], BF16, f"w1_bf{h}") for h in range(2)]
-        dealt = [x[:].rearrange("p (t m j) -> p m t j", t=4, j=PACK) for x in w1_bf]
-        SPLIT = 48
+        w1_bf = tile([P, PACK * H], BF16, "w1_bf")
+        dealt = w1_bf[:].rearrange("p (t m j) -> p m t j", t=4, j=PACK)
+        SPLIT = 40
         src0 = w1_raw[0][:].rearrange("p j (m t) -> p m t j", t=4)
         src1 = w1_raw[1][:].rearrange("p j (m t) -> p m t j", t=4)
-        nc.scalar.copy(dealt[0], src0)
-        nc.vector.tensor_copy(dealt[1][:, 0:SPLIT], src1[:, 0:SPLIT])
-        nc.scalar.copy(dealt[1][:, SPLIT:64], src1[:, SPLIT:64])
+        nc.scalar.copy(dealt[:, 0:64], src0)
+        nc.vector.tensor_copy(dealt[:, 64 : 64 + SPLIT], src1[:, 0:SPLIT])
+        nc.scalar.copy(dealt[:, 64 + SPLIT : 128], src1[:, SPLIT:64])
         w1_code = [tile([P, P], U32, f"w1_code{t}") for t in range(4)]
         w1_scale = [tile([P, P], U8, f"w1_scale{t}") for t in range(4)]
-        for h in range(2):
-            ms = slice(64 * h, 64 * h + 64)
-            for t in range(4):
-                nc.vector.quantize_mx(
-                    w1_code[t][:, ms].bitcast(FP8X4), w1_scale[t][:, ms], w1_bf[h][:, t * HALF : (t + 1) * HALF]
-                )
+        for t in range(4):
+            nc.vector.quantize_mx(w1_code[t][:].bitcast(FP8X4), w1_scale[t][:], w1_bf[:, t * H : (t + 1) * H])
 
+        x_code = tile([P, S], U32, "x_code")
+        for lo, hi in ((0, 1), (1, 2), (2, 4)):
+            nc.vector.tensor_copy(
+                x_code[:, lo * V : hi * V],
+                x_word_tab[:].bitcast(U32).indirect(offsets[:, lo * V // 16 : hi * V // 16]),
+            )
         h_bank = []
         for d in range(PIECES):
             bank = ps.tile([P, 4 * V], F32, name=f"h{d}")
@@ -107,19 +106,16 @@ def tile_picked_statpool_none_po_kernel(
                 )
             h_bank.append(bank[:].rearrange("p (t v) -> p v t", t=4))
 
-        w_code = [tile([P, H], I32, f"w_code{u}") for u in range(2)]
+        w_codes = sb.tile([P, 2 * H], I32, name="w_codes", tag="table_then_codes", align_bytes=64)
+        w_code = [w_codes[:, u * H : (u + 1) * H] for u in range(2)]
         w_scale = tile([P, H], U8, "w_scale")
 
         def deal(dst, src):
-            nc.vector.tensor_copy(
-                dst.rearrange("p (t b i) -> p b t i", t=4, i=4), src.rearrange("p (b i t) -> p b t i", t=4, i=4)
-            )
+            nc.gpsimd.tensor_copy(dst.rearrange("p (t m) -> p t m", t=4), src.rearrange("p (m t) -> p t m", t=4))
 
-        deal(w_code[0][:], w_word_raw[0])
-        deal(w_code[1][:], w_word_raw[1])
-        nc.gpsimd.tensor_copy(
-            w_scale[:].rearrange("p (t m) -> p t m", t=4), w_scale_raw[:].rearrange("p (m t) -> p t m", t=4)
-        )
+        deal(w_code[0], w_word_raw[0])
+        deal(w_code[1], w_word_raw[1])
+        deal(w_scale[:], w_scale_raw[:])
 
         def woven(name, dtype=F32):
             return tile([P, 4 * V], dtype, name)
@@ -131,10 +127,8 @@ def tile_picked_statpool_none_po_kernel(
             nc.vector.scalar_tensor_tensor(vt(out)[:, vs], h_bank[d][:, vs], c, vt(prev)[:, vs], MULT, ADD)
 
         halves = (slice(0, V // 2), slice(V // 2, V))
-        s1, s3 = woven("s1"), woven("s3")
-        pair = sb.tile([P, 8 * V], F32, name="pair", tag="words_then_pair", align_bytes=64)
-        s2, c1 = pair[:, 0 : 4 * V], pair[:, 4 * V : 8 * V]
-        c2, c3 = woven("c2"), woven("c3")
+        s1, s2, s3 = woven("s1"), woven("s2"), woven("s3")
+        c1, c2, c3 = woven("c1"), woven("c2"), woven("c3")
         q1, q2, q3, var = woven("q1"), woven("q2"), woven("q3"), woven("var")
         q12 = sb.tile([P, 4 * V], F32, name="q12", tag="scale_then_sum", align_bytes=64)
         mean_bf, dev_bf = woven("mean_bf", BF16), woven("dev_bf", BF16)

@@ -48,15 +48,15 @@ def tile_picked_statpool_none_po_kernel(
 
         HALF = H // 2
         w1_rows = w1.rearrange("(p j) c -> p j c", j=PACK)
-        w1_raw = [tile([P, PACK, HALF], F32, f"w1_raw{h}") for h in range(2)]
-        nc.sync.dma_start(w1_raw[0][:], w1_rows[:, :, 0:HALF])
+        w1_raw = sb.tile([P, PACK, H], F32, name="w1_raw", tag="raw_then_picked", align_bytes=64)
+        nc.sync.dma_start(w1_raw[:, :, 0:HALF], w1_rows[:, :, 0:HALF])
         nc.sync.dma_start(offsets[:], offs)
         for q in range(QUADS):
             nc.sync.dma_start(
                 x_scale_tab[32 * q : 32 * q + 4, :].bitcast(I32), x_scales[0, 4 * q : 4 * q + 4, :].bitcast(I32)
             )
         nc.scalar.activation(root_two[:], two[:], ACT.Sqrt)
-        nc.sync.dma_start(w1_raw[1][:], w1_rows[:, :, HALF:H])
+        nc.sync.dma_start(w1_raw[:, :, HALF:H], w1_rows[:, :, HALF:H])
         x_word_tab = sb.tile([P, T], I32, name="x_word_tab", tag="table_then_codes", align_bytes=64)
         nc.sync.dma_start(x_word_tab[:], words_of(x_words))
         w_word_raw = [tile([P, H], I32, f"w_word_raw{u}")[:] for u in range(2)]
@@ -74,18 +74,23 @@ def tile_picked_statpool_none_po_kernel(
 
         w1_bf = tile([P, PACK * H], BF16, "w1_bf")
         dealt = w1_bf[:].rearrange("p (t m j) -> p m t j", t=4, j=PACK)
-        SPLIT = 40
-        src0 = w1_raw[0][:].rearrange("p j (m t) -> p m t j", t=4)
-        src1 = w1_raw[1][:].rearrange("p j (m t) -> p m t j", t=4)
-        nc.scalar.copy(dealt[:, 0:64], src0)
-        nc.vector.tensor_copy(dealt[:, 64 : 64 + SPLIT], src1[:, 0:SPLIT])
-        nc.scalar.copy(dealt[:, 64 + SPLIT : 128], src1[:, SPLIT:64])
+        src = w1_raw[:].rearrange("p j (m t) -> p m t j", t=4)
         w1_code = [tile([P, P], U32, f"w1_code{t}") for t in range(4)]
         w1_scale = [tile([P, P], U8, f"w1_scale{t}") for t in range(4)]
-        for t in range(4):
-            nc.vector.quantize_mx(w1_code[t][:].bitcast(FP8X4), w1_scale[t][:], w1_bf[:, t * H : (t + 1) * H])
+        nc.scalar.copy(dealt[:, 0:62], src[:, 0:62])
+        nc.scalar.copy(dealt[:, 62:66], src[:, 62:66])
+        nc.vector.tensor_copy(dealt[:, 66:106], src[:, 66:106])
+        nc.scalar.copy(dealt[:, 106:128], src[:, 106:128])
+        for h in range(2):
+            ms = slice(64 * h, 64 * h + 64)
+            for t in range(4):
+                nc.vector.quantize_mx(
+                    w1_code[t][:, ms].bitcast(FP8X4),
+                    w1_scale[t][:, ms],
+                    w1_bf[:, t * H + h * HALF : t * H + (h + 1) * HALF],
+                )
 
-        x_code = tile([P, S], U32, "x_code")
+        x_code = sb.tile([P, S], U32, name="x_code", tag="raw_then_picked", align_bytes=64)
         for lo, hi in ((0, 1), (1, 2), (2, 4)):
             nc.vector.tensor_copy(
                 x_code[:, lo * V : hi * V],

@@ -15,6 +15,7 @@ FP8X4 = mybir.dt.float8_e4m3fn_x4
 ACT = mybir.ActivationFunctionType
 MULT = mybir.AluOpType.mult
 ADD = mybir.AluOpType.add
+SUB = mybir.AluOpType.subtract
 
 P = 128
 PACK = 4
@@ -32,6 +33,7 @@ def tile_picked_statpool_none_po_kernel(
     nc = tc.nc
     with ExitStack() as ctx:
         sb = ctx.enter_context(tc.tile_pool(name="sb", bufs=1))
+        chain = ctx.enter_context(tc.tile_pool(name="chain", bufs=1))
         ps = ctx.enter_context(tc.psum_pool(name="ps", bufs=1))
 
         def tile(shape, dtype, name):
@@ -39,7 +41,7 @@ def tile_picked_statpool_none_po_kernel(
 
         offsets = sb.tile([P, S // 16], U16, name="offsets")
         x_scale_tab = tile([P, T], U8, "x_scale_tab")
-        w_scale_raw = sb.tile([P, H], U8, name="w_scale_raw", tag="scale_then_sum", align_bytes=64)
+        w_scale_raw = chain.tile([P, H], U8, name="w_scale_raw", offset=1792, align_bytes=64)
         two = tile([P, 1], F32, "two")
         root_two = tile([P, 1], F32, "root_two")
         nc.vector.memset(x_scale_tab[:].bitcast(I32), 0)
@@ -59,15 +61,23 @@ def tile_picked_statpool_none_po_kernel(
         nc.sync.dma_start(w1_raw[:, :, HALF:H], w1_rows[:, :, HALF:H])
         x_word_tab = sb.tile([P, T], I32, name="x_word_tab", tag="table_then_codes", align_bytes=64)
         nc.sync.dma_start(x_word_tab[:], words_of(x_words))
-        w_word_raw = [tile([P, H], I32, f"w_word_raw{u}")[:] for u in range(2)]
-        for u, (words, scales) in enumerate(((w2_words, w2_scales), (w3_words, w3_scales))):
-            nc.sync.dma_start(w_word_raw[u], words_of(words))
-        for u, (words, scales) in enumerate(((w2_words, w2_scales), (w3_words, w3_scales))):
-            for q in range(QUADS):
+        w_word_raw = [
+            sb.tile([P, H], I32, name="w2_word_raw", tag="raw_then_sum", align_bytes=64)[:],
+            tile([P, H], I32, "w3_word_raw")[:],
+        ]
+
+        def load_w_scales(u, scales, quads):
+            for q in quads:
                 r = 32 * q + 4 * u
                 nc.sync.dma_start(
                     w_scale_raw[r : r + 4, :].bitcast(I32), scales[0, 4 * q : 4 * q + 4, :].bitcast(I32)
                 )
+
+        load_w_scales(0, w2_scales, (0, 1))
+        nc.sync.dma_start(w_word_raw[0], words_of(w2_words))
+        nc.sync.dma_start(w_word_raw[1], words_of(w3_words))
+        load_w_scales(0, w2_scales, (2, 3))
+        load_w_scales(1, w3_scales, range(QUADS))
 
         x_scale = tile([P, S], U8, "x_scale")
         nc.vector.tensor_copy(x_scale[:], x_scale_tab[:].indirect(offsets[:]))
@@ -111,14 +121,18 @@ def tile_picked_statpool_none_po_kernel(
                 )
             h_bank.append(bank[:].rearrange("p (t v) -> p v t", t=4))
 
-        w_codes = sb.tile([P, 2 * H], I32, name="w_codes", tag="table_then_codes", align_bytes=64)
-        w_code = [w_codes[:, u * H : (u + 1) * H] for u in range(2)]
+        w_code = [
+            tile([P, H], I32, "w2_code")[:],
+            sb.tile([P, H], I32, name="w3_code", tag="table_then_codes", align_bytes=64)[:],
+        ]
         w_scale = tile([P, H], U8, "w_scale")
 
         def deal(dst, src):
             nc.gpsimd.tensor_copy(dst.rearrange("p (t m) -> p t m", t=4), src.rearrange("p (m t) -> p t m", t=4))
 
-        deal(w_code[0], w_word_raw[0])
+        nc.vector.tensor_copy(
+            w_code[0].rearrange("p (t m) -> p m t", t=4), w_word_raw[0].rearrange("p (m t) -> p m t", t=4)
+        )
         deal(w_code[1], w_word_raw[1])
         deal(w_scale[:], w_scale_raw[:])
 
@@ -132,20 +146,27 @@ def tile_picked_statpool_none_po_kernel(
             nc.vector.scalar_tensor_tensor(vt(out)[:, vs], h_bank[d][:, vs], c, vt(prev)[:, vs], MULT, ADD)
 
         halves = (slice(0, V // 2), slice(V // 2, V))
-        s1, s2, s3 = woven("s1"), woven("s2"), woven("s3")
-        c1, c2, c3 = woven("c1"), woven("c2"), woven("c3")
-        q1, q2, q3, var = woven("q1"), woven("q2"), woven("q3"), woven("var")
-        q12 = sb.tile([P, 4 * V], F32, name="q12", tag="scale_then_sum", align_bytes=64)
+        s1, s3 = woven("s1"), woven("s3")
+        s2 = sb.tile([P, 4 * V], F32, name="s2", tag="raw_then_sum", align_bytes=64)
+        c1a, h0b = tile([P, 2 * V], F32, "c1a"), tile([P, 2 * V], F32, "h0b")
+        c1b = chain.tile([P, 2 * V], F32, name="c1b", offset=1024, align_bytes=64)
+        c2, c3 = woven("c2"), woven("c3")
+        q1, q2, var = woven("q1"), woven("q2"), woven("var")
+        q3 = chain.tile([P, 4 * V], F32, name="q3", offset=0, align_bytes=64)
+        q12 = chain.tile([P, 4 * V], F32, name="q12", offset=2048, align_bytes=64)
         mean_bf, dev_bf = woven("mean_bf", BF16), woven("dev_bf", BF16)
         for vs in halves:
             nc.scalar.activation(vt(s1)[:, vs], h_bank[0][:, vs], ACT.Copy, scale=0.25)
             step(s2, 1, 0.25, s1, vs)
-        for vs in halves:
-            step(c1, 1, -0.25, s1, vs)
-            nc.scalar.activation(vt(q1)[:, vs], vt(c1)[:, vs], ACT.Square, scale=root_two[:])
+        nc.scalar.activation(vt(h0b), h_bank[0][:, halves[1]], ACT.Copy, scale=0.5)
+        nc.vector.scalar_tensor_tensor(vt(c1a), h_bank[1][:, halves[0]], -0.25, vt(s1)[:, halves[0]], MULT, ADD)
+        nc.scalar.activation(q1[:, 0 : 2 * V], c1a[:], ACT.Square, scale=root_two[:])
+        nc.gpsimd.tensor_tensor(c1b[:], h0b[:], s2[:, 2 * V : 4 * V], SUB)
         for vs in halves:
             step(c2, 2, -0.5, s2, vs)
-            nc.scalar.activation(vt(q2)[:, vs], vt(c2)[:, vs], ACT.Square, scale=(2.0 / 3.0) ** 0.5)
+        nc.scalar.activation(q2[:, 0 : 2 * V], c2[:, 0 : 2 * V], ACT.Square, scale=(2.0 / 3.0) ** 0.5)
+        nc.scalar.activation(q2[:, 2 * V : 4 * V], c2[:, 2 * V : 4 * V], ACT.Square, scale=(2.0 / 3.0) ** 0.5)
+        nc.scalar.activation(q1[:, 2 * V : 4 * V], c1b[:], ACT.Square, scale=root_two[:])
         for vs in halves:
             nc.gpsimd.tensor_tensor(vt(q12)[:, vs], vt(q1)[:, vs], vt(q2)[:, vs], ADD)
         for vs in halves:
@@ -158,7 +179,7 @@ def tile_picked_statpool_none_po_kernel(
             nc.vector.tensor_tensor(vt(var)[:, vs], vt(q12)[:, vs], vt(q3)[:, vs], ADD)
             nc.scalar.activation(vt(dev_bf)[:, vs], vt(var)[:, vs], ACT.Sqrt)
         stat_code = [
-            sb.tile([P, V], U32, name="mean_code", tag="scale_then_sum", align_bytes=64),
+            chain.tile([P, V], U32, name="mean_code", offset=3072, align_bytes=64),
             tile([P, V], U32, "dev_code"),
         ]
         stat_scale = [tile([P, V], U8, f"stat_scale{u}") for u in range(2)]

@@ -41,7 +41,7 @@ def tile_picked_statpool_none_po_kernel(
 
         offsets = sb.tile([P, S // 16], U16, name="offsets")
         x_scale_tab = tile([P, T], U8, "x_scale_tab")
-        w_scale_raw = chain.tile([P, H], U8, name="w_scale_raw", offset=1792, align_bytes=64)
+        w_scale_raw = chain.tile([P, H], U8, name="w_scale_raw", offset=0, align_bytes=64)
         two = tile([P, 1], F32, "two")
         root_two = tile([P, 1], F32, "root_two")
         nc.vector.memset(x_scale_tab[:].bitcast(I32), 0)
@@ -50,16 +50,16 @@ def tile_picked_statpool_none_po_kernel(
 
         HALF = H // 2
         w1_rows = w1.rearrange("(p j) c -> p j c", j=PACK)
-        w1_raw = sb.tile([P, PACK, H], F32, name="w1_raw", tag="raw_then_picked", align_bytes=64)
-        nc.sync.dma_start(w1_raw[:, :, 0:HALF], w1_rows[:, :, 0:HALF])
+        w1_raw = sb.tile([P, 2, PACK, HALF], F32, name="w1_raw", tag="raw_then_picked", align_bytes=64)
+        nc.sync.dma_start(w1_raw[:, 0], w1_rows[:, :, 0:HALF])
         nc.sync.dma_start(offsets[:], offs)
         for q in range(QUADS):
             nc.sync.dma_start(
                 x_scale_tab[32 * q : 32 * q + 4, :].bitcast(I32), x_scales[0, 4 * q : 4 * q + 4, :].bitcast(I32)
             )
         nc.scalar.activation(root_two[:], two[:], ACT.Sqrt)
-        nc.sync.dma_start(w1_raw[:, :, HALF:H], w1_rows[:, :, HALF:H])
-        x_word_tab = sb.tile([P, T], I32, name="x_word_tab", tag="table_then_codes", align_bytes=64)
+        nc.sync.dma_start(w1_raw[:, 1], w1_rows[:, :, HALF:H])
+        x_word_tab = tile([P, T], I32, "x_word_tab")
         nc.sync.dma_start(x_word_tab[:], words_of(x_words))
         w_word_raw = [
             sb.tile([P, H], I32, name="w2_word_raw", tag="raw_then_sum", align_bytes=64)[:],
@@ -83,14 +83,15 @@ def tile_picked_statpool_none_po_kernel(
         nc.vector.tensor_copy(x_scale[:], x_scale_tab[:].indirect(offsets[:]))
 
         w1_bf = tile([P, PACK * H], BF16, "w1_bf")
-        dealt = w1_bf[:].rearrange("p (t m j) -> p m t j", t=4, j=PACK)
-        src = w1_raw[:].rearrange("p j (m t) -> p m t j", t=4)
+        dealt = w1_bf[:].rearrange("p (t h m j) -> p h m t j", t=4, h=2, j=PACK)
+        src = w1_raw[:].rearrange("p h j (m t) -> p h m t j", t=4)
         w1_code = [tile([P, P], U32, f"w1_code{t}") for t in range(4)]
         w1_scale = [tile([P, P], U8, f"w1_scale{t}") for t in range(4)]
-        nc.scalar.copy(dealt[:, 0:62], src[:, 0:62])
-        nc.scalar.copy(dealt[:, 62:66], src[:, 62:66])
-        nc.vector.tensor_copy(dealt[:, 66:106], src[:, 66:106])
-        nc.scalar.copy(dealt[:, 106:128], src[:, 106:128])
+        nc.vector.tensor_copy(dealt[:, 0, 0:12], src[:, 0, 0:12])
+        nc.scalar.copy(dealt[:, 0, 12:62], src[:, 0, 12:62])
+        nc.scalar.copy(dealt[:, :, 62:64], src[:, :, 62:64])
+        nc.vector.tensor_copy(dealt[:, 1, 0:44], src[:, 1, 0:44])
+        nc.scalar.copy(dealt[:, 1, 44:62], src[:, 1, 44:62])
         for h in range(2):
             ms = slice(64 * h, 64 * h + 64)
             for t in range(4):
@@ -123,17 +124,18 @@ def tile_picked_statpool_none_po_kernel(
 
         w_code = [
             tile([P, H], I32, "w2_code")[:],
-            sb.tile([P, H], I32, name="w3_code", tag="table_then_codes", align_bytes=64)[:],
         ]
         w_scale = tile([P, H], U8, "w_scale")
 
         def deal(dst, src):
             nc.gpsimd.tensor_copy(dst.rearrange("p (t m) -> p t m", t=4), src.rearrange("p (m t) -> p t m", t=4))
 
-        nc.vector.tensor_copy(
-            w_code[0].rearrange("p (t m) -> p m t", t=4), w_word_raw[0].rearrange("p (m t) -> p m t", t=4)
-        )
-        deal(w_code[1], w_word_raw[1])
+        def deal_words(u):
+            nc.vector.tensor_copy(
+                w_code[u].rearrange("p (t m) -> p m t", t=4), w_word_raw[u].rearrange("p (m t) -> p m t", t=4)
+            )
+
+        deal_words(0)
         deal(w_scale[:], w_scale_raw[:])
 
         def woven(name, dtype=F32):
@@ -148,42 +150,51 @@ def tile_picked_statpool_none_po_kernel(
         halves = (slice(0, V // 2), slice(V // 2, V))
         s1, s3 = woven("s1"), woven("s3")
         s2 = sb.tile([P, 4 * V], F32, name="s2", tag="raw_then_sum", align_bytes=64)
-        c1a, h0b = tile([P, 2 * V], F32, "c1a"), tile([P, 2 * V], F32, "h0b")
-        c1b = chain.tile([P, 2 * V], F32, name="c1b", offset=1024, align_bytes=64)
+        h0 = [
+            sb.tile([P, 2 * V], F32, name="h0_0", tag="h0_then_q2", align_bytes=64),
+            sb.tile([P, 2 * V], F32, name="h0_1", tag="h0_then_q3", align_bytes=64),
+        ]
+        c1 = chain.tile([P, 4 * V], F32, name="c1", offset=0, align_bytes=64)
         c2, c3 = woven("c2"), woven("c3")
-        q1, q2, var = woven("q1"), woven("q2"), woven("var")
-        q3 = chain.tile([P, 4 * V], F32, name="q3", offset=0, align_bytes=64)
-        q12 = chain.tile([P, 4 * V], F32, name="q12", offset=2048, align_bytes=64)
+        q1, var = woven("q1"), woven("var")
+        q12 = [chain.tile([P, 2 * V], F32, name=f"q12_{h}", offset=2048 + 1024 * h, align_bytes=64) for h in range(2)]
         mean_bf, dev_bf = woven("mean_bf", BF16), woven("dev_bf", BF16)
+        cols = (slice(0, 2 * V), slice(2 * V, 4 * V))
         for vs in halves:
             nc.scalar.activation(vt(s1)[:, vs], h_bank[0][:, vs], ACT.Copy, scale=0.25)
             step(s2, 1, 0.25, s1, vs)
-        nc.scalar.activation(vt(h0b), h_bank[0][:, halves[1]], ACT.Copy, scale=0.5)
-        nc.vector.scalar_tensor_tensor(vt(c1a), h_bank[1][:, halves[0]], -0.25, vt(s1)[:, halves[0]], MULT, ADD)
-        nc.scalar.activation(q1[:, 0 : 2 * V], c1a[:], ACT.Square, scale=root_two[:])
-        nc.gpsimd.tensor_tensor(c1b[:], h0b[:], s2[:, 2 * V : 4 * V], SUB)
-        for vs in halves:
-            step(c2, 2, -0.5, s2, vs)
-        nc.scalar.activation(q2[:, 0 : 2 * V], c2[:, 0 : 2 * V], ACT.Square, scale=(2.0 / 3.0) ** 0.5)
-        nc.scalar.activation(q2[:, 2 * V : 4 * V], c2[:, 2 * V : 4 * V], ACT.Square, scale=(2.0 / 3.0) ** 0.5)
-        nc.scalar.activation(q1[:, 2 * V : 4 * V], c1b[:], ACT.Square, scale=root_two[:])
-        for vs in halves:
-            nc.gpsimd.tensor_tensor(vt(q12)[:, vs], vt(q1)[:, vs], vt(q2)[:, vs], ADD)
-        for vs in halves:
-            step(s3, 2, 0.25, s2, vs)
-        for vs in halves:
+        for h, (vs, cs) in enumerate(zip(halves, cols)):
+            nc.scalar.activation(vt(h0[h]), h_bank[0][:, vs], ACT.Copy, scale=0.5)
+            nc.gpsimd.tensor_tensor(c1[:, cs], h0[h][:], s2[:, cs], SUB)
+        q2 = [
+            tile([P, 2 * V], F32, "q2_0"),
+            sb.tile([P, 2 * V], F32, name="q2_1", tag="h0_then_q2", align_bytes=64),
+        ]
+        step(c2, 2, -0.5, s2, halves[0])
+        step(s3, 2, 0.25, s2)
+        step(c2, 2, -0.5, s2, halves[1])
+        nc.scalar.activation(q2[0][:], c2[:, cols[0]], ACT.Square, scale=(2.0 / 3.0) ** 0.5)
+        nc.scalar.activation(q1[:, cols[0]], c1[:, cols[0]], ACT.Square, scale=root_two[:])
+        nc.scalar.activation(q2[1][:], c2[:, cols[1]], ACT.Square, scale=(2.0 / 3.0) ** 0.5)
+        nc.scalar.activation(q1[:, cols[1]], c1[:, cols[1]], ACT.Square, scale=root_two[:])
+        nc.gpsimd.tensor_tensor(q12[0][:], q1[:, cols[0]], q2[0][:], ADD)
+        q3 = sb.tile([P, 4 * V], F32, name="q3", tag="h0_then_q3", align_bytes=64)
+        for vs, cs in zip(halves, cols):
             step(c3, 3, -0.75, s3, vs)
-            nc.scalar.activation(vt(q3)[:, vs], vt(c3)[:, vs], ACT.Square, scale=(1.0 / 3.0) ** 0.5)
+            nc.scalar.activation(q3[:, cs], c3[:, cs], ACT.Square, scale=(1.0 / 3.0) ** 0.5)
         step(mean_bf, 3, 0.25, s3)
-        for vs in halves:
-            nc.vector.tensor_tensor(vt(var)[:, vs], vt(q12)[:, vs], vt(q3)[:, vs], ADD)
-            nc.scalar.activation(vt(dev_bf)[:, vs], vt(var)[:, vs], ACT.Sqrt)
+        nc.vector.tensor_tensor(q12[1][:], q1[:, cols[1]], q2[1][:], ADD)
+        for h, cs in enumerate(cols):
+            nc.vector.tensor_tensor(var[:, cs], q12[h][:], q3[:, cs], ADD)
+            nc.scalar.activation(dev_bf[:, cs], var[:, cs], ACT.Sqrt)
         stat_code = [
-            chain.tile([P, V], U32, name="mean_code", offset=3072, align_bytes=64),
+            chain.tile([P, V], U32, name="mean_code", offset=2048, align_bytes=64),
             tile([P, V], U32, "dev_code"),
         ]
+        w_code.append(chain.tile([P, H], I32, name="w3_code", offset=3072, align_bytes=64)[:])
         stat_scale = [tile([P, V], U8, f"stat_scale{u}") for u in range(2)]
         nc.vector.quantize_mx(stat_code[0][:].bitcast(FP8X4), stat_scale[0][:], mean_bf[:])
+        deal_words(1)
         for vs in halves:
             nc.vector.quantize_mx(
                 stat_code[1][:, vs].bitcast(FP8X4), stat_scale[1][:, vs], dev_bf[:, 4 * vs.start : 4 * vs.stop]

@@ -62,7 +62,7 @@ def tile_picked_statpool_none_po_kernel(
         x_word_tab = tile([P, T], I32, "x_word_tab")
         nc.sync.dma_start(x_word_tab[:], words_of(x_words))
         w_word_raw = [
-            sb.tile([P, H], I32, name="w2_word_raw", tag="raw_then_sum", align_bytes=64)[:],
+            chain.tile([P, H], I32, name="w2_word_raw", offset=5120, align_bytes=64)[:],
             tile([P, H], I32, "w3_word_raw")[:],
         ]
 
@@ -73,11 +73,11 @@ def tile_picked_statpool_none_po_kernel(
                     w_scale_raw[r : r + 4, :].bitcast(I32), scales[0, 4 * q : 4 * q + 4, :].bitcast(I32)
                 )
 
-        load_w_scales(0, w2_scales, (0, 1))
+        load_w_scales(0, w2_scales, (0,))
         nc.sync.dma_start(w_word_raw[0], words_of(w2_words))
-        nc.sync.dma_start(w_word_raw[1], words_of(w3_words))
-        load_w_scales(0, w2_scales, (2, 3))
+        load_w_scales(0, w2_scales, (1, 2, 3))
         load_w_scales(1, w3_scales, range(QUADS))
+        nc.sync.dma_start(w_word_raw[1], words_of(w3_words))
 
         x_scale = tile([P, S], U8, "x_scale")
         nc.vector.tensor_copy(x_scale[:], x_scale_tab[:].indirect(offsets[:]))
@@ -125,7 +125,7 @@ def tile_picked_statpool_none_po_kernel(
         w_code = [
             tile([P, H], I32, "w2_code")[:],
         ]
-        w_scale = tile([P, H], U8, "w_scale")
+        w_scale = chain.tile([P, H], U8, name="w_scale", offset=5120, align_bytes=64)
 
         def deal(dst, src):
             nc.gpsimd.tensor_copy(dst.rearrange("p (t m) -> p t m", t=4), src.rearrange("p (m t) -> p t m", t=4))
@@ -149,7 +149,7 @@ def tile_picked_statpool_none_po_kernel(
 
         halves = (slice(0, V // 2), slice(V // 2, V))
         s1, s3 = woven("s1"), woven("s3")
-        s2 = sb.tile([P, 4 * V], F32, name="s2", tag="raw_then_sum", align_bytes=64)
+        s2 = chain.tile([P, 4 * V], F32, name="s2", offset=5632, align_bytes=64)
         h0 = [
             sb.tile([P, 2 * V], F32, name="h0_0", tag="h0_then_q2", align_bytes=64),
             sb.tile([P, 2 * V], F32, name="h0_1", tag="h0_then_q3", align_bytes=64),

@@ -41,7 +41,7 @@ def tile_picked_statpool_none_po_kernel(
 
         offsets = sb.tile([P, S // 16], U16, name="offsets")
         x_scale_tab = tile([P, T], U8, "x_scale_tab")
-        w_scale_raw = chain.tile([P, H], U8, name="w_scale_raw", offset=0, align_bytes=64)
+        w_scale_raw = chain.tile([P, H], U8, name="w_scale_raw", offset=1024, align_bytes=64)
         two = tile([P, 1], F32, "two")
         root_two = tile([P, 1], F32, "root_two")
         nc.vector.memset(x_scale_tab[:].bitcast(I32), 0)
@@ -107,20 +107,36 @@ def tile_picked_statpool_none_po_kernel(
                 x_code[:, lo * V : hi * V],
                 x_word_tab[:].bitcast(U32).indirect(offsets[:, lo * V // 16 : hi * V // 16]),
             )
-        h_bank = []
-        for d in range(PIECES):
-            bank = ps.tile([P, 4 * V], F32, name=f"h{d}")
-            for t in range(4):
-                nc.tensor.matmul_mx(
-                    bank[:, t * V : (t + 1) * V],
-                    lhsT=w1_code[t][:].bitcast(FP8X4),
-                    lhsT_scale=w1_scale[t][:],
-                    rhs=x_code[:, d * V : (d + 1) * V].bitcast(FP8X4),
-                    rhs_scale=x_scale[:, d * V : (d + 1) * V],
-                    start=True,
-                    stop=True,
-                )
-            h_bank.append(bank[:].rearrange("p (t v) -> p v t", t=4))
+
+        def product(name, parts):
+            bank = ps.tile([P, 4 * V], F32, name=name, tag=name)
+            for i, (t, pieces) in enumerate(parts):
+                for n, d in enumerate(pieces):
+                    nc.tensor.matmul_mx(
+                        bank[:, i * V : (i + 1) * V],
+                        lhsT=w1_code[t][:].bitcast(FP8X4),
+                        lhsT_scale=w1_scale[t][:],
+                        rhs=x_code[:, d * V : (d + 1) * V].bitcast(FP8X4),
+                        rhs_scale=x_scale[:, d * V : (d + 1) * V],
+                        start=(n == 0),
+                        stop=(n == len(pieces) - 1),
+                    )
+            return bank[:, 0 : len(parts) * V]
+
+        def low(*pieces):
+            return [(t, pieces) for t in (0, 1)]
+
+        def high(*pieces):
+            return [(t, pieces) for t in (2, 3)]
+
+        h0_lo = product("h0_lo", low(0))
+        h1_lo = product("h1_lo", low(1))
+        h1_hi = product("h1_hi", high(1))
+        h2_lo = product("h2_lo", low(2))
+        h01_hi = product("h01_hi", high(0, 1))
+        h3_hi = product("h3_hi", high(3))
+        last = product("last", low(3) + high(2, 3))
+        h3_lo, h23_hi = last[:, 0 : 2 * V], last[:, 2 * V : 4 * V]
 
         w_code = [
             tile([P, H], I32, "w2_code")[:],
@@ -135,63 +151,84 @@ def tile_picked_statpool_none_po_kernel(
                 w_code[u].rearrange("p (t m) -> p m t", t=4), w_word_raw[u].rearrange("p (m t) -> p m t", t=4)
             )
 
-        deal_words(0)
+        deal(w_code[0], w_word_raw[0])
         deal(w_scale[:], w_scale_raw[:])
 
         def woven(name, dtype=F32):
             return tile([P, 4 * V], dtype, name)
 
-        def vt(x):
-            return x[:, :].rearrange("p (v t) -> p v t", t=4)
+        def step(out, bank, c, prev):
+            nc.vector.scalar_tensor_tensor(out, bank, c, prev, MULT, ADD)
 
-        def step(out, d, c, prev, vs=slice(0, V)):
-            nc.vector.scalar_tensor_tensor(vt(out)[:, vs], h_bank[d][:, vs], c, vt(prev)[:, vs], MULT, ADD)
+        def half(name, offset=None, width=2 * V):
+            if offset is None:
+                return tile([P, width], F32, name)[:]
+            return chain.tile([P, width], F32, name=name, offset=offset, align_bytes=64)[:]
 
+        def square(q, c, scale):
+            nc.scalar.activation(q, c, ACT.Square, scale=scale)
+
+        LO, HI = slice(0, 2 * V), slice(2 * V, 4 * V)
         halves = (slice(0, V // 2), slice(V // 2, V))
-        s1, s3 = woven("s1"), woven("s3")
-        s2 = chain.tile([P, 4 * V], F32, name="s2", offset=5632, align_bytes=64)
-        h0 = [
-            sb.tile([P, 2 * V], F32, name="h0_0", tag="h0_then_q2", align_bytes=64),
-            sb.tile([P, 2 * V], F32, name="h0_1", tag="h0_then_q3", align_bytes=64),
-        ]
-        c1 = chain.tile([P, 4 * V], F32, name="c1", offset=0, align_bytes=64)
-        c2, c3 = woven("c2"), woven("c3")
-        q1, var = woven("q1"), woven("var")
-        q12 = [chain.tile([P, 2 * V], F32, name=f"q12_{h}", offset=2048 + 1024 * h, align_bytes=64) for h in range(2)]
-        mean_bf, dev_bf = woven("mean_bf", BF16), woven("dev_bf", BF16)
-        cols = (slice(0, 2 * V), slice(2 * V, 4 * V))
+        dev_bf = woven("dev_bf", BF16)
+        mean_bf = chain.tile([P, 4 * V], BF16, name="mean_bf", offset=256, align_bytes=64)
+        h0 = half("h0")
+        nc.scalar.activation(h0, h0_lo, ACT.Copy)
+        first = half("first", 8192, 4 * V)
+        s2, c1 = first[:, LO], first[:, HI]
+        c2, c3, b, d, e, q2, qb, qe = (half(n) for n in ("c2", "c3", "b", "d", "e", "q2", "qb", "qe"))
+        q1 = half("q1", 12288)
+        step(s2, h1_lo, 1.0, h0)
+        step(c1, h1_lo, -1.0, h0)
+        square(q1, c1, root_two[:])
+        sums = half("sums", None, 4 * V)
+        s3, s01 = sums[:, LO], sums[:, HI]
+        nc.scalar.activation(s01, h01_hi, ACT.Copy)
+        step(c2, h2_lo, -2.0, s2)
+        step(s3, h2_lo, 1.0, s2)
+        square(q2, c2, (2.0 / 3.0) ** 0.5)
+        h3_twice = half("h3_twice", 8192)
+        nc.scalar.activation(h3_twice, h3_hi, ACT.Copy, scale=-2.0)
+        q_first = half("q_first", 1280, 4 * V)
+        q12, qbe = q_first[:, LO], q_first[:, HI]
+        q_last, var = half("q_last", None, 4 * V), half("var", None, 4 * V)
+        nc.gpsimd.tensor_tensor(q12, q1, q2, ADD)
+        step(b, h1_hi, -2.0, s01)
+        square(qb, b, root_two[:])
+        step(e, h23_hi, -1.0, s01)
+        square(qe, e, 1.0)
+        step(c3, h3_lo, -3.0, s3)
+        square(q_last[:, LO], c3, (1.0 / 3.0) ** 0.5)
+        step(d, h23_hi, 1.0, h3_twice)
+        square(q_last[:, HI], d, root_two[:])
+
+        def tv(x):
+            return x.rearrange("p (t v) -> p t v", t=4)
+
+        def mean(h):
+            vs = halves[h]
+            step(
+                mean_bf[:].rearrange("p (v t) -> p v t", t=4)[:, vs],
+                last.rearrange("p (t v) -> p v t", t=4)[:, vs],
+                1.0,
+                sums.rearrange("p (t v) -> p v t", t=4)[:, vs],
+            )
+
+        mean(0)
+        nc.vector.tensor_tensor(qbe, qb, qe, ADD)
+        mean(1)
         for vs in halves:
-            nc.scalar.activation(vt(s1)[:, vs], h_bank[0][:, vs], ACT.Copy, scale=0.25)
-            step(s2, 1, 0.25, s1, vs)
-        for h, (vs, cs) in enumerate(zip(halves, cols)):
-            nc.scalar.activation(vt(h0[h]), h_bank[0][:, vs], ACT.Copy, scale=0.5)
-            nc.gpsimd.tensor_tensor(c1[:, cs], h0[h][:], s2[:, cs], SUB)
-        q2 = [
-            tile([P, 2 * V], F32, "q2_0"),
-            sb.tile([P, 2 * V], F32, name="q2_1", tag="h0_then_q2", align_bytes=64),
-        ]
-        step(c2, 2, -0.5, s2, halves[0])
-        step(s3, 2, 0.25, s2)
-        step(c2, 2, -0.5, s2, halves[1])
-        nc.scalar.activation(q2[0][:], c2[:, cols[0]], ACT.Square, scale=(2.0 / 3.0) ** 0.5)
-        nc.scalar.activation(q1[:, cols[0]], c1[:, cols[0]], ACT.Square, scale=root_two[:])
-        nc.scalar.activation(q2[1][:], c2[:, cols[1]], ACT.Square, scale=(2.0 / 3.0) ** 0.5)
-        nc.scalar.activation(q1[:, cols[1]], c1[:, cols[1]], ACT.Square, scale=root_two[:])
-        nc.gpsimd.tensor_tensor(q12[0][:], q1[:, cols[0]], q2[0][:], ADD)
-        q3 = sb.tile([P, 4 * V], F32, name="q3", tag="h0_then_q3", align_bytes=64)
-        for vs, cs in zip(halves, cols):
-            step(c3, 3, -0.75, s3, vs)
-            nc.scalar.activation(q3[:, cs], c3[:, cs], ACT.Square, scale=(1.0 / 3.0) ** 0.5)
-        step(mean_bf, 3, 0.25, s3)
-        nc.vector.tensor_tensor(q12[1][:], q1[:, cols[1]], q2[1][:], ADD)
-        for h, cs in enumerate(cols):
-            nc.vector.tensor_tensor(var[:, cs], q12[h][:], q3[:, cs], ADD)
-            nc.scalar.activation(dev_bf[:, cs], var[:, cs], ACT.Sqrt)
+            nc.vector.tensor_tensor(tv(var)[:, :, vs], tv(q_first)[:, :, vs], tv(q_last)[:, :, vs], ADD)
+            nc.scalar.activation(
+                dev_bf[:, 4 * vs.start : 4 * vs.stop].rearrange("p (c i t) -> p c t i", i=4, t=4),
+                tv(var)[:, :, vs].rearrange("p t (c i) -> p c t i", i=4),
+                ACT.Sqrt,
+            )
         stat_code = [
-            chain.tile([P, V], U32, name="mean_code", offset=2048, align_bytes=64),
+            chain.tile([P, V], U32, name="mean_code", offset=12288, align_bytes=64),
             tile([P, V], U32, "dev_code"),
         ]
-        w_code.append(chain.tile([P, H], I32, name="w3_code", offset=3072, align_bytes=64)[:])
+        w_code.append(chain.tile([P, H], I32, name="w3_code", offset=2048, align_bytes=64)[:])
         stat_scale = [tile([P, V], U8, f"stat_scale{u}") for u in range(2)]
         nc.vector.quantize_mx(stat_code[0][:].bitcast(FP8X4), stat_scale[0][:], mean_bf[:])
         deal_words(1)
@@ -200,7 +237,7 @@ def tile_picked_statpool_none_po_kernel(
                 stat_code[1][:, vs].bitcast(FP8X4), stat_scale[1][:, vs], dev_bf[:, 4 * vs.start : 4 * vs.stop]
             )
 
-        y_bank = [ps.tile([P, V], F32, name=f"y{t}") for t in range(4)]
+        y_bank = [ps.tile([P, V], F32, name=f"y{t}", tag=tag) for t, tag in enumerate(("h0_lo", "h1_lo", "h2_lo", "h1_hi"))]
         y = tile([P, 4, V], F32, "y")
         for u in range(2):
             for t in range(4):
@@ -214,7 +251,7 @@ def tile_picked_statpool_none_po_kernel(
                     stop=(u == 1),
                 )
         for t in range(4):
-            nc.scalar.copy(y[:, t, :], y_bank[t][:])
+            nc.scalar.activation(y[:, t, :], y_bank[t][:], ACT.Copy, scale=0.25)
         nc.scalar.dma_start(out_0.rearrange("(p t) v -> p t v", t=4), y[:])
 
         y_bf = woven("y_bf", BF16)

@@ -62,7 +62,8 @@ def tile_picked_statpool_none_po_kernel(
         x_word_tab = tile([P, T], I32, "x_word_tab")
         nc.sync.dma_start(x_word_tab[:], words_of(x_words))
         w_word_raw = [
-            chain.tile([P, H], I32, name="w2_word_raw", offset=5120, align_bytes=64)[:],
+            chain.tile([P, HALF], I32, name="w2_word_raw0", offset=5120, align_bytes=64)[:],
+            tile([P, HALF], I32, "w2_word_raw1")[:],
             tile([P, H], I32, "w3_word_raw")[:],
         ]
 
@@ -74,10 +75,11 @@ def tile_picked_statpool_none_po_kernel(
                 )
 
         load_w_scales(0, w2_scales, (0,))
-        nc.sync.dma_start(w_word_raw[0], words_of(w2_words))
+        nc.sync.dma_start(w_word_raw[0], words_of(w2_words)[:, 0:HALF])
+        nc.sync.dma_start(w_word_raw[1], words_of(w2_words)[:, HALF:H])
         load_w_scales(0, w2_scales, (1, 2, 3))
         load_w_scales(1, w3_scales, range(QUADS))
-        nc.sync.dma_start(w_word_raw[1], words_of(w3_words))
+        nc.sync.dma_start(w_word_raw[2], words_of(w3_words))
 
         x_scale = tile([P, S], U8, "x_scale")
         nc.vector.tensor_copy(x_scale[:], x_scale_tab[:].indirect(offsets[:]))
@@ -146,12 +148,13 @@ def tile_picked_statpool_none_po_kernel(
         def deal(dst, src):
             nc.gpsimd.tensor_copy(dst.rearrange("p (t m) -> p t m", t=4), src.rearrange("p (m t) -> p t m", t=4))
 
-        def deal_words(u):
+        def deal_words(dst, raw, lo, hi):
             nc.vector.tensor_copy(
-                w_code[u].rearrange("p (t m) -> p m t", t=4), w_word_raw[u].rearrange("p (m t) -> p m t", t=4)
+                dst.rearrange("p (t m) -> p m t", t=4)[:, lo:hi], raw.rearrange("p (m t) -> p m t", t=4)
             )
 
-        deal(w_code[0], w_word_raw[0])
+        deal_words(w_code[0], w_word_raw[0], 0, 64)
+        deal_words(w_code[0], w_word_raw[1], 64, 128)
         deal(w_scale[:], w_scale_raw[:])
 
         def woven(name, dtype=F32):
@@ -174,7 +177,7 @@ def tile_picked_statpool_none_po_kernel(
         mean_bf = chain.tile([P, 4 * V], BF16, name="mean_bf", offset=256, align_bytes=64)
         h0 = half("h0")
         nc.scalar.activation(h0, h0_lo, ACT.Copy)
-        first = half("first", 8192, 4 * V)
+        first = half("first", 5632, 4 * V)
         s2, c1 = first[:, LO], first[:, HI]
         c2, c3, b, d, e, q2, qb, qe = (half(n) for n in ("c2", "c3", "b", "d", "e", "q2", "qb", "qe"))
         q1 = half("q1", 12288)
@@ -187,7 +190,7 @@ def tile_picked_statpool_none_po_kernel(
         step(c2, h2_lo, -2.0, s2)
         step(s3, h2_lo, 1.0, s2)
         square(q2, c2, (2.0 / 3.0) ** 0.5)
-        h3_twice = half("h3_twice", 8192)
+        h3_twice = half("h3_twice", 5632)
         nc.scalar.activation(h3_twice, h3_hi, ACT.Copy, scale=-2.0)
         q_first = half("q_first", 1280, 4 * V)
         q12, qbe = q_first[:, LO], q_first[:, HI]
@@ -231,7 +234,7 @@ def tile_picked_statpool_none_po_kernel(
         w_code.append(chain.tile([P, H], I32, name="w3_code", offset=2048, align_bytes=64)[:])
         stat_scale = [tile([P, V], U8, f"stat_scale{u}") for u in range(2)]
         nc.vector.quantize_mx(stat_code[0][:].bitcast(FP8X4), stat_scale[0][:], mean_bf[:])
-        deal_words(1)
+        deal_words(w_code[1], w_word_raw[2], 0, 128)
         for vs in halves:
             nc.vector.quantize_mx(
                 stat_code[1][:, vs].bitcast(FP8X4), stat_scale[1][:, vs], dev_bf[:, 4 * vs.start : 4 * vs.stop]

@@ -220,7 +220,7 @@ def tile_picked_statpool_none_po_kernel(
         mean(0)
         nc.vector.tensor_tensor(qbe, qb, qe, ADD)
         mean(1)
-        for vs in halves:
+        for vs in (slice(n * V // 4, (n + 1) * V // 4) for n in range(4)):
             nc.vector.tensor_tensor(tv(var)[:, :, vs], tv(q_first)[:, :, vs], tv(q_last)[:, :, vs], ADD)
             nc.scalar.activation(
                 dev_bf[:, 4 * vs.start : 4 * vs.stop].rearrange("p (c i t) -> p c t i", i=4, t=4),
@@ -253,8 +253,10 @@ def tile_picked_statpool_none_po_kernel(
                     start=(u == 0),
                     stop=(u == 1),
                 )
-        for t in range(4):
+        for t in range(3):
             nc.scalar.activation(y[:, t, :], y_bank[t][:], ACT.Copy, scale=0.25)
+        for vs in halves:
+            nc.scalar.activation(y[:, 3, vs], y_bank[3][:, vs], ACT.Copy, scale=0.25)
         nc.scalar.dma_start(out_0.rearrange("(p t) v -> p t v", t=4), y[:])
 
         y_bf = woven("y_bf", BF16)

@@ -131,7 +131,7 @@ def tile_picked_statpool_none_po_kernel(
         def high(*pieces):
             return [(t, pieces) for t in (2, 3)]
 
-        h0_lo = product("h0_lo", low(0))
+        h0_lo = [product(f"h0_{t}", [(t, (0,))]) for t in range(2)]
         h1_lo = product("h1_lo", low(1))
         h1_hi = product("h1_hi", high(1))
         h2_lo = product("h2_lo", low(2))
@@ -176,7 +176,8 @@ def tile_picked_statpool_none_po_kernel(
         dev_bf = woven("dev_bf", BF16)
         mean_bf = chain.tile([P, 4 * V], BF16, name="mean_bf", offset=256, align_bytes=64)
         h0 = half("h0")
-        nc.scalar.activation(h0, h0_lo, ACT.Copy)
+        for t in range(2):
+            nc.scalar.activation(h0[:, t * V : (t + 1) * V], h0_lo[t], ACT.Copy)
         first = half("first", 5632, 4 * V)
         s2, c1 = first[:, LO], first[:, HI]
         c2, c3, b, d, e, q2, qb, qe = (half(n) for n in ("c2", "c3", "b", "d", "e", "q2", "qb", "qe"))
@@ -208,14 +209,15 @@ def tile_picked_statpool_none_po_kernel(
         def tv(x):
             return x.rearrange("p (t v) -> p t v", t=4)
 
+        def weave_out(x, vs):
+            return x[:, 4 * vs.start : 4 * vs.stop].rearrange("p (c i t) -> p c t i", i=4, t=4)
+
+        def weave_in(x, vs):
+            return tv(x)[:, :, vs].rearrange("p t (c i) -> p c t i", i=4)
+
         def mean(h):
             vs = halves[h]
-            step(
-                mean_bf[:].rearrange("p (v t) -> p v t", t=4)[:, vs],
-                last.rearrange("p (t v) -> p v t", t=4)[:, vs],
-                1.0,
-                sums.rearrange("p (t v) -> p v t", t=4)[:, vs],
-            )
+            nc.vector.tensor_tensor(weave_out(mean_bf, vs), weave_in(last, vs), weave_in(sums, vs), ADD)
 
         mean(0)
         nc.vector.tensor_tensor(qbe, qb, qe, ADD)
@@ -240,7 +242,7 @@ def tile_picked_statpool_none_po_kernel(
                 stat_code[1][:, vs].bitcast(FP8X4), stat_scale[1][:, vs], dev_bf[:, 4 * vs.start : 4 * vs.stop]
             )
 
-        y_bank = [ps.tile([P, V], F32, name=f"y{t}", tag=tag) for t, tag in enumerate(("h0_lo", "h1_lo", "h2_lo", "h1_hi"))]
+        y_bank = [ps.tile([P, V], F32, name=f"y{t}", tag=tag) for t, tag in enumerate(("h0_0", "h0_1", "h2_lo", "h1_hi"))]
         y = tile([P, 4, V], F32, "y")
         for u in range(2):
             for t in range(4):

@@ -59,11 +59,11 @@ def tile_picked_statpool_none_po_kernel(
             )
         nc.scalar.activation(root_two[:], two[:], ACT.Sqrt)
         nc.sync.dma_start(w1_raw[:, 1], w1_rows[:, :, HALF:H])
-        x_word_tab = tile([P, T], I32, "x_word_tab")
+        x_word_tab = chain.tile([P, T], I32, name="x_word_tab", offset=16384, align_bytes=64)
         nc.sync.dma_start(x_word_tab[:], words_of(x_words))
         w_word_raw = [
-            chain.tile([P, HALF], I32, name="w2_word_raw0", offset=5120, align_bytes=64)[:],
-            tile([P, HALF], I32, "w2_word_raw1")[:],
+            tile([P, HALF], I32, "w2_word_raw0")[:],
+            chain.tile([P, HALF], I32, name="w2_word_raw1", offset=9216, align_bytes=64)[:],
             tile([P, H], I32, "w3_word_raw")[:],
         ]
 
@@ -133,17 +133,17 @@ def tile_picked_statpool_none_po_kernel(
 
         h0_lo = [product(f"h0_{t}", [(t, (0,))]) for t in range(2)]
         h1_lo = product("h1_lo", low(1))
-        h1_hi = product("h1_hi", high(1))
-        h2_lo = product("h2_lo", low(2))
         h01_hi = product("h01_hi", high(0, 1))
-        h3_hi = product("h3_hi", high(3))
+        h2_lo = product("h2_lo", low(2))
+        h1_hi = product("h1_hi", high(1))
         last = product("last", low(3) + high(2, 3))
+        h3_hi = product("h3_hi", high(3))
         h3_lo, h23_hi = last[:, 0 : 2 * V], last[:, 2 * V : 4 * V]
 
         w_code = [
-            tile([P, H], I32, "w2_code")[:],
+            chain.tile([P, H], I32, name="w2_code", offset=16384, align_bytes=64)[:],
         ]
-        w_scale = chain.tile([P, H], U8, name="w_scale", offset=5120, align_bytes=64)
+        w_scale = tile([P, H], U8, "w_scale")
 
         def deal(dst, src):
             nc.gpsimd.tensor_copy(dst.rearrange("p (t m) -> p t m", t=4), src.rearrange("p (m t) -> p t m", t=4))
@@ -153,8 +153,10 @@ def tile_picked_statpool_none_po_kernel(
                 dst.rearrange("p (t m) -> p m t", t=4)[:, lo:hi], raw.rearrange("p (m t) -> p m t", t=4)
             )
 
-        deal_words(w_code[0], w_word_raw[0], 0, 64)
-        deal_words(w_code[0], w_word_raw[1], 64, 128)
+        nc.gpsimd.tensor_copy(
+            w_code[0].bitcast(U32).rearrange("p (t m) -> p t m", t=4)[:, :, 0:64],
+            w_word_raw[0].bitcast(U32).rearrange("p (m t) -> p t m", t=4),
+        )
         deal(w_scale[:], w_scale_raw[:])
 
         def woven(name, dtype=F32):
@@ -178,16 +180,24 @@ def tile_picked_statpool_none_po_kernel(
         h0 = half("h0")
         for t in range(2):
             nc.scalar.activation(h0[:, t * V : (t + 1) * V], h0_lo[t], ACT.Copy)
+        nc.scalar.copy(
+            w_code[0].bitcast(U32).rearrange("p (t m) -> p m t", t=4)[:, 64:128],
+            w_word_raw[1].bitcast(U32).rearrange("p (m t) -> p m t", t=4),
+        )
         first = half("first", 5632, 4 * V)
         s2, c1 = first[:, LO], first[:, HI]
-        c2, c3, b, d, e, q2, qb, qe = (half(n) for n in ("c2", "c3", "b", "d", "e", "q2", "qb", "qe"))
-        q1 = half("q1", 12288)
+        c2, c3, d, qb = (half(n) for n in ("c2", "c3", "d", "qb"))
+        q_low = half("q_low", 9728, 4 * V)
+        q1, q2 = q_low[:, LO], q_low[:, HI]
+        high_first = half("high_first", None, 4 * V)
+        b, e = high_first[:, LO], high_first[:, HI]
+        qe = half("qe")
         step(s2, h1_lo, 1.0, h0)
         step(c1, h1_lo, -1.0, h0)
-        square(q1, c1, root_two[:])
-        sums = half("sums", None, 4 * V)
+        sums = half("sums", 7680, 4 * V)
         s3, s01 = sums[:, LO], sums[:, HI]
         nc.scalar.activation(s01, h01_hi, ACT.Copy)
+        square(q1, c1, root_two[:])
         step(c2, h2_lo, -2.0, s2)
         step(s3, h2_lo, 1.0, s2)
         square(q2, c2, (2.0 / 3.0) ** 0.5)
@@ -230,7 +240,7 @@ def tile_picked_statpool_none_po_kernel(
                 ACT.Sqrt,
             )
         stat_code = [
-            chain.tile([P, V], U32, name="mean_code", offset=12288, align_bytes=64),
+            chain.tile([P, V], U32, name="mean_code", offset=10752, align_bytes=64),
             tile([P, V], U32, "dev_code"),
         ]
         w_code.append(chain.tile([P, H], I32, name="w3_code", offset=2048, align_bytes=64)[:])

@@ -85,30 +85,43 @@ def tile_picked_statpool_none_po_kernel(
         nc.vector.tensor_copy(x_scale[:], x_scale_tab[:].indirect(offsets[:]))
 
         w1_bf = tile([P, PACK * H], BF16, "w1_bf")
+        w1_codes, w1_scales = tile([P, H], U32, "w1_codes"), tile([P, H], U8, "w1_scales")
+        w1_code = [w1_codes[:, t * P : (t + 1) * P] for t in range(4)]
+        w1_scale = [w1_scales[:, t * P : (t + 1) * P] for t in range(4)]
+
         dealt = w1_bf[:].rearrange("p (t h m j) -> p h m t j", t=4, h=2, j=PACK)
         src = w1_raw[:].rearrange("p h j (m t) -> p h m t j", t=4)
-        w1_code = [tile([P, P], U32, f"w1_code{t}") for t in range(4)]
-        w1_scale = [tile([P, P], U8, f"w1_scale{t}") for t in range(4)]
-        nc.vector.tensor_copy(dealt[:, 0, 0:12], src[:, 0, 0:12])
-        nc.scalar.copy(dealt[:, 0, 12:62], src[:, 0, 12:62])
-        nc.scalar.copy(dealt[:, :, 62:64], src[:, :, 62:64])
-        nc.vector.tensor_copy(dealt[:, 1, 0:44], src[:, 1, 0:44])
-        nc.scalar.copy(dealt[:, 1, 44:62], src[:, 1, 44:62])
-        for h in range(2):
-            ms = slice(64 * h, 64 * h + 64)
-            for t in range(4):
-                nc.vector.quantize_mx(
-                    w1_code[t][:, ms].bitcast(FP8X4),
-                    w1_scale[t][:, ms],
-                    w1_bf[:, t * H + h * HALF : t * H + (h + 1) * HALF],
-                )
+
+        def round_w1(copy, h, ms, ts):
+            copy(dealt[:, h, ms, ts], src[:, h, ms, ts])
+
+        ALL_T, LOW_T, HIGH_T = slice(0, 4), slice(0, 2), slice(2, 4)
+        round_w1(nc.vector.tensor_copy, 0, slice(0, 20), ALL_T)
+        round_w1(nc.scalar.copy, 0, slice(20, 62), ALL_T)
+        round_w1(nc.scalar.copy, slice(0, 2), slice(62, 64), ALL_T)
+        round_w1(nc.vector.tensor_copy, 1, slice(0, 62), LOW_T)
+        round_w1(nc.scalar.copy, 1, slice(0, 62), HIGH_T)
 
         x_code = sb.tile([P, S], U32, name="x_code", tag="raw_then_picked", align_bytes=64)
-        for lo, hi in ((0, 1), (1, 2), (2, 4)):
+
+        def quantise_w1(h, t):
+            ms = slice(64 * h, 64 * h + 64)
+            lo = t * H + h * HALF
+            nc.vector.quantize_mx(w1_code[t][:, ms].bitcast(FP8X4), w1_scale[t][:, ms], w1_bf[:, lo : lo + HALF])
+
+        def pick_words(lo, hi):
             nc.vector.tensor_copy(
                 x_code[:, lo * V : hi * V],
                 x_word_tab[:].bitcast(U32).indirect(offsets[:, lo * V // 16 : hi * V // 16]),
             )
+
+        for h, t in ((0, 0), (0, 1), (1, 0), (1, 1)):
+            quantise_w1(h, t)
+        pick_words(0, 1)
+        pick_words(1, 2)
+        nc.vector.quantize_mx(w1_codes[:, HALF:H].bitcast(FP8X4), w1_scales[:, HALF:H], w1_bf[:, 2 * H : 4 * H])
+        pick_words(2, 3)
+        pick_words(3, 4)
 
         def product(name, parts):
             bank = ps.tile([P, 4 * V], F32, name=name, tag=name)
@@ -116,8 +129,8 @@ def tile_picked_statpool_none_po_kernel(
                 for n, d in enumerate(pieces):
                     nc.tensor.matmul_mx(
                         bank[:, i * V : (i + 1) * V],
-                        lhsT=w1_code[t][:].bitcast(FP8X4),
-                        lhsT_scale=w1_scale[t][:],
+                        lhsT=w1_code[t].bitcast(FP8X4),
+                        lhsT_scale=w1_scale[t],
                         rhs=x_code[:, d * V : (d + 1) * V].bitcast(FP8X4),
                         rhs_scale=x_scale[:, d * V : (d + 1) * V],
                         start=(n == 0),
@@ -133,8 +146,9 @@ def tile_picked_statpool_none_po_kernel(
 
         h0_lo = [product(f"h0_{t}", [(t, (0,))]) for t in range(2)]
         h1_lo = product("h1_lo", low(1))
-        h01_hi = product("h01_hi", high(0, 1))
+        h01_hi = [product("h01_hi", [(2, (0, 1))])]
         h2_lo = product("h2_lo", low(2))
+        h01_hi.append(product("h0_0", [(3, (0, 1))]))
         h1_hi = product("h1_hi", high(1))
         last = product("last", low(3) + high(2, 3))
         h3_hi = product("h3_hi", high(3))
@@ -196,7 +210,8 @@ def tile_picked_statpool_none_po_kernel(
         step(c1, h1_lo, -1.0, h0)
         sums = half("sums", 7680, 4 * V)
         s3, s01 = sums[:, LO], sums[:, HI]
-        nc.scalar.activation(s01, h01_hi, ACT.Copy)
+        nc.scalar.activation(s01[:, 0:V], h01_hi[0], ACT.Copy)
+        nc.scalar.activation(s01[:, V : 2 * V], h01_hi[1], ACT.Copy)
         square(q1, c1, root_two[:])
         step(c2, h2_lo, -2.0, s2)
         step(s3, h2_lo, 1.0, s2)

@@ -102,6 +102,19 @@ def tile_picked_statpool_none_po_kernel(
         round_w1(nc.vector.tensor_copy, 1, slice(0, 62), LOW_T)
         round_w1(nc.scalar.copy, 1, slice(0, 62), HIGH_T)
 
+        def warm_up(passes):
+            bank = ps.tile([P, V], F32, name="warm_up", tag="h3_hi")
+            for n in range(passes):
+                nc.tensor.matmul_mx(
+                    bank[0:32, :],
+                    lhsT=w1_code[0][:, 0:32].bitcast(FP8X4),
+                    lhsT_scale=w1_scale[0][:, 0:32],
+                    rhs=w1_code[0].bitcast(FP8X4),
+                    rhs_scale=w1_scale[0],
+                    start=True,
+                    stop=True,
+                )
+
         x_code = sb.tile([P, S], U32, name="x_code", tag="raw_then_picked", align_bytes=64)
 
         def quantise_w1(h, t):
@@ -117,6 +130,7 @@ def tile_picked_statpool_none_po_kernel(
 
         for h, t in ((0, 0), (0, 1), (1, 0), (1, 1)):
             quantise_w1(h, t)
+        warm_up(6)
         pick_words(0, 1)
         pick_words(1, 2)
         nc.vector.quantize_mx(w1_codes[:, HALF:H].bitcast(FP8X4), w1_scales[:, HALF:H], w1_bf[:, 2 * H : 4 * H])

@@ -131,11 +131,9 @@ def tile_picked_statpool_none_po_kernel(
         for h, t in ((0, 0), (0, 1), (1, 0), (1, 1)):
             quantise_w1(h, t)
         warm_up(6)
-        pick_words(0, 1)
-        pick_words(1, 2)
         nc.vector.quantize_mx(w1_codes[:, HALF:H].bitcast(FP8X4), w1_scales[:, HALF:H], w1_bf[:, 2 * H : 4 * H])
-        pick_words(2, 3)
-        pick_words(3, 4)
+        for piece in range(PIECES):
+            pick_words(piece, piece + 1)
 
         def product(name, parts):
             bank = ps.tile([P, 4 * V], F32, name=name, tag=name)

@@ -130,7 +130,7 @@ def tile_picked_statpool_none_po_kernel(
 
         for h, t in ((0, 0), (0, 1), (1, 0), (1, 1)):
             quantise_w1(h, t)
-        warm_up(6)
+        warm_up(5)
         nc.vector.quantize_mx(w1_codes[:, HALF:H].bitcast(FP8X4), w1_scales[:, HALF:H], w1_bf[:, 2 * H : 4 * H])
         for piece in range(PIECES):
             pick_words(piece, piece + 1)

from contextlib import ExitStack

import concourse.mybir as mybir

K, T, S, V, H = 512, 1024, 512, 128, 512
FLOPS = 2 * K * H * S + 2 * 2 * H * H * V

F32 = mybir.dt.float32
BF16 = mybir.dt.bfloat16
I32 = mybir.dt.int32
U32 = mybir.dt.uint32
U16 = mybir.dt.uint16
U8 = mybir.dt.uint8
FP8X4 = mybir.dt.float8_e4m3fn_x4
ACT = mybir.ActivationFunctionType
MULT = mybir.AluOpType.mult
ADD = mybir.AluOpType.add
SUB = mybir.AluOpType.subtract

P = 128
PACK = 4
PIECES = 4
QUADS = 4


def words_of(dram):
    return dram[0].rearrange("p n r -> p (n r)").bitcast(I32)


def tile_picked_statpool_none_po_kernel(
    tc, x_words, x_scales, w1, w2_words, w2_scales, w3_words, w3_scales, offs, out_0, out_1, out_2
):
    nc = tc.nc
    with ExitStack() as ctx:
        sb = ctx.enter_context(tc.tile_pool(name="sb", bufs=1))
        chain = ctx.enter_context(tc.tile_pool(name="chain", bufs=1))
        ps = ctx.enter_context(tc.psum_pool(name="ps", bufs=1))

        def tile(shape, dtype, name):
            return sb.tile(shape, dtype, name=name, align_bytes=64)

        offsets = sb.tile([P, S // 16], U16, name="offsets")
        x_scale_tab = tile([P, T], U8, "x_scale_tab")
        w_scale_raw = chain.tile([P, H], U8, name="w_scale_raw", offset=1024, align_bytes=64)
        two = tile([P, 1], F32, "two")
        root_two = tile([P, 1], F32, "root_two")
        nc.vector.memset(x_scale_tab[:].bitcast(I32), 0)
        nc.vector.memset(two[:], 2.0)
        nc.vector.memset(w_scale_raw[:].bitcast(I32), 0)

        HALF = H // 2
        w1_rows = w1.rearrange("(p j) c -> p j c", j=PACK)
        w1_raw = sb.tile([P, 2, PACK, HALF], F32, name="w1_raw", tag="raw_then_picked", align_bytes=64)
        nc.sync.dma_start(w1_raw[:, 0], w1_rows[:, :, 0:HALF])
        nc.sync.dma_start(offsets[:], offs)
        for q in range(QUADS):
            nc.sync.dma_start(
                x_scale_tab[32 * q : 32 * q + 4, :].bitcast(I32), x_scales[0, 4 * q : 4 * q + 4, :].bitcast(I32)
            )
        nc.scalar.activation(root_two[:], two[:], ACT.Sqrt)
        nc.sync.dma_start(w1_raw[:, 1], w1_rows[:, :, HALF:H])
        x_word_tab = chain.tile([P, T], I32, name="x_word_tab", offset=16384, align_bytes=64)
        nc.sync.dma_start(x_word_tab[:], words_of(x_words))
        w_word_raw = [
            tile([P, HALF], I32, "w2_word_raw0")[:],
            chain.tile([P, HALF], I32, name="w2_word_raw1", offset=9216, align_bytes=64)[:],
            tile([P, H], I32, "w3_word_raw")[:],
        ]

        def load_w_scales(u, scales, quads):
            for q in quads:
                r = 32 * q + 4 * u
                nc.sync.dma_start(
                    w_scale_raw[r : r + 4, :].bitcast(I32), scales[0, 4 * q : 4 * q + 4, :].bitcast(I32)
                )

        load_w_scales(0, w2_scales, (0,))
        nc.sync.dma_start(w_word_raw[0], words_of(w2_words)[:, 0:HALF])
        nc.sync.dma_start(w_word_raw[1], words_of(w2_words)[:, HALF:H])
        load_w_scales(0, w2_scales, (1, 2, 3))
        load_w_scales(1, w3_scales, range(QUADS))
        nc.sync.dma_start(w_word_raw[2], words_of(w3_words))

        x_scale = tile([P, S], U8, "x_scale")
        nc.vector.tensor_copy(x_scale[:], x_scale_tab[:].indirect(offsets[:]))

        w1_bf = tile([P, PACK * H], BF16, "w1_bf")
        w1_codes, w1_scales = tile([P, H], U32, "w1_codes"), tile([P, H], U8, "w1_scales")
        w1_code = [w1_codes[:, t * P : (t + 1) * P] for t in range(4)]
        w1_scale = [w1_scales[:, t * P : (t + 1) * P] for t in range(4)]

        dealt = w1_bf[:].rearrange("p (t h m j) -> p h m t j", t=4, h=2, j=PACK)
        src = w1_raw[:].rearrange("p h j (m t) -> p h m t j", t=4)

        def round_w1(copy, h, ms, ts):
            copy(dealt[:, h, ms, ts], src[:, h, ms, ts])

        ALL_T, LOW_T, HIGH_T = slice(0, 4), slice(0, 2), slice(2, 4)
        round_w1(nc.vector.tensor_copy, 0, slice(0, 20), ALL_T)
        round_w1(nc.scalar.copy, 0, slice(20, 62), ALL_T)
        round_w1(nc.scalar.copy, slice(0, 2), slice(62, 64), ALL_T)
        round_w1(nc.vector.tensor_copy, 1, slice(0, 62), LOW_T)
        round_w1(nc.scalar.copy, 1, slice(0, 62), HIGH_T)

        def warm_up(passes):
            bank = ps.tile([P, V], F32, name="warm_up", tag="h3_hi")
            for n in range(passes):
                nc.tensor.matmul_mx(
                    bank[0:32, :],
                    lhsT=w1_code[0][:, 0:32].bitcast(FP8X4),
                    lhsT_scale=w1_scale[0][:, 0:32],
                    rhs=w1_code[0].bitcast(FP8X4),
                    rhs_scale=w1_scale[0],
                    start=True,
                    stop=True,
                )

        x_code = sb.tile([P, S], U32, name="x_code", tag="raw_then_picked", align_bytes=64)

        def quantise_w1(h, t):
            ms = slice(64 * h, 64 * h + 64)
            lo = t * H + h * HALF
            nc.vector.quantize_mx(w1_code[t][:, ms].bitcast(FP8X4), w1_scale[t][:, ms], w1_bf[:, lo : lo + HALF])

        def pick_words(lo, hi):
            nc.vector.tensor_copy(
                x_code[:, lo * V : hi * V],
                x_word_tab[:].bitcast(U32).indirect(offsets[:, lo * V // 16 : hi * V // 16]),
            )

        for h, t in ((0, 0), (0, 1), (1, 0), (1, 1)):
            quantise_w1(h, t)
        warm_up(5)
        nc.vector.quantize_mx(w1_codes[:, HALF:H].bitcast(FP8X4), w1_scales[:, HALF:H], w1_bf[:, 2 * H : 4 * H])
        for piece in range(PIECES):
            pick_words(piece, piece + 1)

        def product(name, parts):
            bank = ps.tile([P, 4 * V], F32, name=name, tag=name)
            for i, (t, pieces) in enumerate(parts):
                for n, d in enumerate(pieces):
                    nc.tensor.matmul_mx(
                        bank[:, i * V : (i + 1) * V],
                        lhsT=w1_code[t].bitcast(FP8X4),
                        lhsT_scale=w1_scale[t],
                        rhs=x_code[:, d * V : (d + 1) * V].bitcast(FP8X4),
                        rhs_scale=x_scale[:, d * V : (d + 1) * V],
                        start=(n == 0),
                        stop=(n == len(pieces) - 1),
                    )
            return bank[:, 0 : len(parts) * V]

        def low(*pieces):
            return [(t, pieces) for t in (0, 1)]

        def high(*pieces):
            return [(t, pieces) for t in (2, 3)]

        h0_lo = [product(f"h0_{t}", [(t, (0,))]) for t in range(2)]
        h1_lo = product("h1_lo", low(1))
        h01_hi = [product("h01_hi", [(2, (0, 1))])]
        h2_lo = product("h2_lo", low(2))
        h01_hi.append(product("h0_0", [(3, (0, 1))]))
        h1_hi = product("h1_hi", high(1))
        last = product("last", low(3) + high(2, 3))
        h3_hi = product("h3_hi", high(3))
        h3_lo, h23_hi = last[:, 0 : 2 * V], last[:, 2 * V : 4 * V]

        w_code = [
            chain.tile([P, H], I32, name="w2_code", offset=16384, align_bytes=64)[:],
        ]
        w_scale = tile([P, H], U8, "w_scale")

        def deal(dst, src):
            nc.gpsimd.tensor_copy(dst.rearrange("p (t m) -> p t m", t=4), src.rearrange("p (m t) -> p t m", t=4))

        def deal_words(dst, raw, lo, hi):
            nc.vector.tensor_copy(
                dst.rearrange("p (t m) -> p m t", t=4)[:, lo:hi], raw.rearrange("p (m t) -> p m t", t=4)
            )

        nc.gpsimd.tensor_copy(
            w_code[0].bitcast(U32).rearrange("p (t m) -> p t m", t=4)[:, :, 0:64],
            w_word_raw[0].bitcast(U32).rearrange("p (m t) -> p t m", t=4),
        )
        deal(w_scale[:], w_scale_raw[:])

        def woven(name, dtype=F32):
            return tile([P, 4 * V], dtype, name)

        def step(out, bank, c, prev):
            nc.vector.scalar_tensor_tensor(out, bank, c, prev, MULT, ADD)

        def half(name, offset=None, width=2 * V):
            if offset is None:
                return tile([P, width], F32, name)[:]
            return chain.tile([P, width], F32, name=name, offset=offset, align_bytes=64)[:]

        def square(q, c, scale):
            nc.scalar.activation(q, c, ACT.Square, scale=scale)

        LO, HI = slice(0, 2 * V), slice(2 * V, 4 * V)
        halves = (slice(0, V // 2), slice(V // 2, V))
        dev_bf = woven("dev_bf", BF16)
        mean_bf = chain.tile([P, 4 * V], BF16, name="mean_bf", offset=256, align_bytes=64)
        h0 = half("h0")
        for t in range(2):
            nc.scalar.activation(h0[:, t * V : (t + 1) * V], h0_lo[t], ACT.Copy)
        nc.scalar.copy(
            w_code[0].bitcast(U32).rearrange("p (t m) -> p m t", t=4)[:, 64:128],
            w_word_raw[1].bitcast(U32).rearrange("p (m t) -> p m t", t=4),
        )
        first = half("first", 5632, 4 * V)
        s2, c1 = first[:, LO], first[:, HI]
        c2, c3, d, qb = (half(n) for n in ("c2", "c3", "d", "qb"))
        q_low = half("q_low", 9728, 4 * V)
        q1, q2 = q_low[:, LO], q_low[:, HI]
        high_first = half("high_first", None, 4 * V)
        b, e = high_first[:, LO], high_first[:, HI]
        qe = half("qe")
        step(s2, h1_lo, 1.0, h0)
        step(c1, h1_lo, -1.0, h0)
        sums = half("sums", 7680, 4 * V)
        s3, s01 = sums[:, LO], sums[:, HI]
        nc.scalar.activation(s01[:, 0:V], h01_hi[0], ACT.Copy)
        nc.scalar.activation(s01[:, V : 2 * V], h01_hi[1], ACT.Copy)
        square(q1, c1, root_two[:])
        step(c2, h2_lo, -2.0, s2)
        step(s3, h2_lo, 1.0, s2)
        square(q2, c2, (2.0 / 3.0) ** 0.5)
        h3_twice = half("h3_twice", 5632)
        nc.scalar.activation(h3_twice, h3_hi, ACT.Copy, scale=-2.0)
        q_first = half("q_first", 1280, 4 * V)
        q12, qbe = q_first[:, LO], q_first[:, HI]
        q_last, var = half("q_last", None, 4 * V), half("var", None, 4 * V)
        nc.gpsimd.tensor_tensor(q12, q1, q2, ADD)
        step(b, h1_hi, -2.0, s01)
        square(qb, b, root_two[:])
        step(e, h23_hi, -1.0, s01)
        square(qe, e, 1.0)
        step(c3, h3_lo, -3.0, s3)
        square(q_last[:, LO], c3, (1.0 / 3.0) ** 0.5)
        step(d, h23_hi, 1.0, h3_twice)
        square(q_last[:, HI], d, root_two[:])

        def tv(x):
            return x.rearrange("p (t v) -> p t v", t=4)

        def weave_out(x, vs):
            return x[:, 4 * vs.start : 4 * vs.stop].rearrange("p (c i t) -> p c t i", i=4, t=4)

        def weave_in(x, vs):
            return tv(x)[:, :, vs].rearrange("p t (c i) -> p c t i", i=4)

        def mean(h):
            vs = halves[h]
            nc.vector.tensor_tensor(weave_out(mean_bf, vs), weave_in(last, vs), weave_in(sums, vs), ADD)

        mean(0)
        nc.vector.tensor_tensor(qbe, qb, qe, ADD)
        mean(1)
        for vs in (slice(n * V // 4, (n + 1) * V // 4) for n in range(4)):
            nc.vector.tensor_tensor(tv(var)[:, :, vs], tv(q_first)[:, :, vs], tv(q_last)[:, :, vs], ADD)
            nc.scalar.activation(
                dev_bf[:, 4 * vs.start : 4 * vs.stop].rearrange("p (c i t) -> p c t i", i=4, t=4),
                tv(var)[:, :, vs].rearrange("p t (c i) -> p c t i", i=4),
                ACT.Sqrt,
            )
        stat_code = [
            chain.tile([P, V], U32, name="mean_code", offset=10752, align_bytes=64),
            tile([P, V], U32, "dev_code"),
        ]
        w_code.append(chain.tile([P, H], I32, name="w3_code", offset=2048, align_bytes=64)[:])
        stat_scale = [tile([P, V], U8, f"stat_scale{u}") for u in range(2)]
        nc.vector.quantize_mx(stat_code[0][:].bitcast(FP8X4), stat_scale[0][:], mean_bf[:])
        deal_words(w_code[1], w_word_raw[2], 0, 128)
        for vs in halves:
            nc.vector.quantize_mx(
                stat_code[1][:, vs].bitcast(FP8X4), stat_scale[1][:, vs], dev_bf[:, 4 * vs.start : 4 * vs.stop]
            )

        y_bank = [ps.tile([P, V], F32, name=f"y{t}", tag=tag) for t, tag in enumerate(("h0_0", "h0_1", "h2_lo", "h1_hi"))]
        y = tile([P, 4, V], F32, "y")
        for u in range(2):
            for t in range(4):
                nc.tensor.matmul_mx(
                    y_bank[t][:],
                    lhsT=w_code[u][:, t * P : (t + 1) * P].bitcast(FP8X4),
                    lhsT_scale=w_scale[4 * u : P, t * P : (t + 1) * P],
                    rhs=stat_code[u][:].bitcast(FP8X4),
                    rhs_scale=stat_scale[u][:],
                    start=(u == 0),
                    stop=(u == 1),
                )
        for t in range(3):
            nc.scalar.activation(y[:, t, :], y_bank[t][:], ACT.Copy, scale=0.25)
        for vs in halves:
            nc.scalar.activation(y[:, 3, vs], y_bank[3][:, vs], ACT.Copy, scale=0.25)
        nc.scalar.dma_start(out_0.rearrange("(p t) v -> p t v", t=4), y[:])

        y_bf = woven("y_bf", BF16)
        for vs in halves:
            nc.vector.tensor_copy(
                y_bf[:, 4 * vs.start : 4 * vs.stop].rearrange("p (c i t) -> p c t i", i=4, t=4),
                y[:, :, vs].rearrange("p t (c i) -> p c t i", i=4),
            )
        y_code = tile([P, V], I32, "y_code")
        y_scale = tile([P, V], U8, "y_scale")
        for vs in halves:
            nc.vector.quantize_mx(
                y_code[:, vs].bitcast(FP8X4), y_scale[:, vs], y_bf[:, 4 * vs.start : 4 * vs.stop]
            )
        nc.sync.dma_start(words_of(out_1), y_code[:])
        for q in range(QUADS):
            eng = nc.sync if q < 2 else nc.scalar
            eng.dma_start(out_2[0, 4 * q : 4 * q + 4, :].bitcast(I32), y_scale[32 * q : 32 * q + 4, :].bitcast(I32))
